import numpy as np
import ml_dtypes


def mxq(x, axis, fmt="e4m3"):
    dtype, down = {"e4m3": (ml_dtypes.float8_e4m3fn, 7), "e5m2": (ml_dtypes.float8_e5m2, 14)}[fmt]
    v = np.moveaxis(np.asarray(x, np.float32).astype(ml_dtypes.bfloat16).astype(np.float64), axis, -1)
    blocks = v.reshape(v.shape[:-1] + (-1, 32))
    amax = np.abs(blocks).max(-1, keepdims=True)
    byte = np.maximum(np.where(amax > 0, np.frexp(amax)[1] - 1 + 127, 0) - down, 1)
    scale = np.exp2(byte - 127.0)
    codes = (blocks / scale).astype(np.float32).astype(dtype).astype(np.float64)
    return np.moveaxis((codes * scale).reshape(v.shape), -1, axis)


WIDE = False


def mx_kscale(k):
    if not WIDE:
        return np.ones(k)
    levels = np.array([10, -10, 5, -5, 0])
    if k % 512:
        return np.exp2(np.random.permutation(np.resize(levels, k // 32))).repeat(32)
    a = np.empty((k // 512, 16))
    for p in range(k // 512):
        a[p, :8] = np.random.permutation(np.resize(levels, 8))
        for g in range(8):
            far = levels[np.abs(levels - a[p, g]) >= 10]
            a[p, g + 8] = far[np.random.randint(len(far))]
    return np.exp2(a.ravel()).repeat(32)


def f64(x):
    return np.asarray(x).astype(np.float64)


def striped(idx):
    return np.tile(idx.reshape(-1, 16).T, (8, 1)).astype(np.uint16)


def unstriped(offs):
    return offs[:16].T.reshape(-1).astype(np.int64)


K, T, E, C, N = 1024, 512, 8, 128, 512
M = 256


def by_expert(wq, xq):
    return np.concatenate([wq[e].T @ xq[:, e * C:(e + 1) * C] for e in range(E)], axis=1)


def setup_inputs():
    n = np.random.standard_normal
    s = mx_kscale(K)[:, None]
    v = mx_kscale(N)
    first = np.random.permutation(np.repeat(np.arange(E), T // E))
    second = (first + 1 + np.random.permutation(np.repeat(np.arange(E - 1), -(-T // (E - 1)))[:T])) % E
    while np.bincount(second, minlength=E).max() != T // E:
        load = np.bincount(second, minlength=E); hi, lo = int(load.argmax()), int(load.argmin())
        t = np.flatnonzero((second == hi) & (first != lo))[0]; second[t] = lo
    slot_token = np.empty(E * C, np.int64); pos = np.empty((2, T), np.int64); fill = np.zeros(E, np.int64)
    place = np.stack([np.random.permutation(C) for _ in range(E)])
    for r, deal in enumerate((first, second)):
        for t in np.random.permutation(T):
            e = deal[t]; j = e * C + place[e, fill[e]]; fill[e] += 1; slot_token[j] = t; pos[r, t] = j
    g = np.random.uniform(0.2, 0.8, T)
    return {
        "xT": (n((K, T)) * s).astype(np.float32),
        "w": (n((E, K, N)) / np.sqrt(K) / s[None] * v[None, None, :]).astype(np.float32),
        "b": (0.3 * n((N, E)) * v[:, None]).astype(np.float32),
        "wp": (n((N, M)) / np.sqrt(N) / v[:, None]).astype(np.float32),
        "gate": np.stack([np.tile(g, (N, 1)), np.tile(1.0 - g, (N, 1))]).astype(np.float32),
        "offs": striped(slot_token),
        "pos1": striped(pos[0]),
        "pos2": striped(pos[1]),
    }


def reference(xT, w, b, wp, gate, offs, pos1, pos2):
    idx = unstriped(offs)
    xq = mxq(f64(xT)[:, idx], 0, "e4m3")
    y = by_expert(mxq(f64(w), 1, "e4m3"), xq)
    y = y + np.repeat(f64(b), C, axis=1)
    c = f64(gate[0]) * y[:, unstriped(pos1)] + f64(gate[1]) * y[:, unstriped(pos2)]
    return mxq(f64(wp), 0, "e4m3").T @ mxq(c, 0, "e4m3")

@@ -1,0 +1,258 @@
+from contextlib import ExitStack
+
+import concourse.mybir as mybir
+
+K, T, E, C, N, M = 1024, 512, 8, 128, 512, 256
+SLOTS = E * C
+
+FLOPS = 2 * SLOTS * K * N + 2 * T * N * M
+BYTES = 4 * (K * T + E * K * N + N * E + N * M + 2 * T + M * T) + 2 * 8 * 16 * (SLOTS + 2 * T) // 16
+
+F32 = mybir.dt.float32
+BF16 = mybir.dt.bfloat16
+U32 = mybir.dt.uint32
+U16 = mybir.dt.uint16
+U8 = mybir.dt.uint8
+FP8X4 = mybir.dt.float8_e4m3fn_x4
+MULT = mybir.AluOpType.mult
+ADD = mybir.AluOpType.add
+IDENTITY = mybir.ActivationFunctionType.Identity
+
+P = 128
+PACK = 4
+K_PASS = P * PACK
+PASSES = K // K_PASS
+R = N // P
+LINE = 4
+SLABS = E * PASSES
+
+X_TOKENS_VECTOR = 352
+W_COLUMNS_VECTOR = [48] * (SLABS - 2) + [80] * 2
+
+SLOT_PIECES = [(0, 256), (256, 640), (640, 1024)]
+
+EXPERT_GROUPS = [(0, 4, "vector"), (4, 2, "vector"), (6, 2, "scalar")]
+
+TOKEN_PIECES = [(0, 256), (256, 384), (384, 512)]
+
+
+def interleave(grouped, raw):
+    return (
+        grouped.rearrange("p (c i j) -> p c j i", i=LINE, j=PACK),
+        raw.rearrange("p j (c i) -> p c j i", i=LINE),
+    )
+
+
+def tile_moe_nxt_lin_bias_kernel(
+    tc, xT, w, b, wp, gate, offs, pos1, pos2, out
+):
+    nc = tc.nc
+    with ExitStack() as ctx:
+        held = ctx.enter_context(tc.tile_pool(name="held", bufs=1))
+        slab_pool = ctx.enter_context(tc.tile_pool(name="slab_pool", bufs=12))
+        cast_pool = ctx.enter_context(tc.tile_pool(name="cast_pool", bufs=4))
+        code_pool = ctx.enter_context(tc.tile_pool(name="code_pool", bufs=6))
+        banks = ctx.enter_context(tc.psum_pool(name="banks", bufs=1))
+
+        offs_sb = held.tile([P, SLOTS // 16], U16, name="offs_sb")
+        pos_sb = [held.tile([P, T // 16], U16, name=f"pos_sb{i}") for i in range(2)]
+
+        x_scales = held.tile([P, T], U8, name="x_scales", align_bytes=64)
+        nc.gpsimd.memset(x_scales[:], 0)
+
+        x_raw = [held.tile([P, PACK, T], F32, name=f"x_raw{a}") for a in range(PASSES)]
+        x_cast = [held.tile([P, T * PACK], BF16, name=f"x_cast{a}", align_bytes=64) for a in range(PASSES)]
+        x_codes = [held.tile([P, T], U32, name=f"x_codes{a}", align_bytes=64) for a in range(PASSES)]
+        slot_codes = [held.tile([P, SLOTS], U32, name=f"slot_codes{a}", align_bytes=64) for a in range(PASSES)]
+        slot_scales = held.tile([P, SLOTS], U8, name="slot_scales", align_bytes=64)
+        b_sb = held.tile([P, R, E], F32, name="b_sb")
+        gate_sb = [held.tile([P, T], F32, name=f"gate_sb{i}") for i in range(2)]
+        wp_raw = held.tile([P, PACK, M], F32, name="wp_raw")
+        wp_cast = held.tile([P, M * PACK], BF16, name="wp_cast", align_bytes=64)
+        wp_codes = held.tile([P, M], U32, name="wp_codes", align_bytes=64)
+        wp_scales = held.tile([P, M], U8, name="wp_scales", align_bytes=64)
+        y = [held.tile([P, SLOTS], F32, name=f"y{r}") for r in range(R)]
+
+        def load_x(a):
+            rows = xT[a * K_PASS : (a + 1) * K_PASS, :]
+            nc.sync.dma_start(out=x_raw[a][:], in_=rows.rearrange("(p j) t -> p j t", j=PACK))
+
+        def quantise_x(a):
+            nc.vector.quantize_mx(
+                out=x_codes[a][:].bitcast(FP8X4), scales=x_scales[4 * a : P, :], in_=x_cast[a][:]
+            )
+
+        def gather_codes(a, slot_piece):
+            lo, hi = SLOT_PIECES[slot_piece]
+            offsets = offs_sb[:, lo // 16 : hi // 16]
+            nc.vector.tensor_copy(out=slot_codes[a][:, lo:hi], in_=x_codes[a][:].indirect(offsets))
+
+        def gather_scales(slot_piece):
+            lo, hi = SLOT_PIECES[slot_piece]
+            offsets = offs_sb[:, lo // 16 : hi // 16]
+            nc.vector.tensor_copy(out=slot_scales[:, lo:hi], in_=x_scales[:].indirect(offsets))
+
+        def load_slab(slab):
+            e, a = divmod(slab, PASSES)
+            raw = slab_pool.tile([P, PACK, N], F32, name="w_raw")
+            rows = w[e, a * K_PASS : (a + 1) * K_PASS, :]
+            nc.sync.dma_start(out=raw[:], in_=rows.rearrange("(p j) n -> p j n", j=PACK))
+            return raw
+
+        def cast_slab(slab, raw):
+            grouped = cast_pool.tile([P, N * PACK], BF16, name="w_cast", align_bytes=64)
+            dst = grouped[:].rearrange("p (r m j) -> p m j r", r=R, j=PACK)
+            src = raw[:].rearrange("p j (m r) -> p m j r", r=R)
+            split = W_COLUMNS_VECTOR[slab]
+            parts = 2 if slab == SLABS - 1 else 1
+            for copy, lo, hi in ((nc.vector.tensor_copy, 0, split), (nc.scalar.copy, split, P)):
+                for part in range(parts):
+                    rs = slice(part * R // parts, (part + 1) * R // parts)
+                    copy(out=dst[:, lo:hi, :, rs], in_=src[:, lo:hi, :, rs])
+            return grouped
+
+        def quantise_slab(slab, grouped):
+            codes = code_pool.tile([P, N], U32, name="w_codes", align_bytes=64)
+            scales = code_pool.tile([P, N], U8, name="w_scales", align_bytes=64)
+            parts = R if slab == SLABS - 1 else 1
+            for part in range(parts):
+                lo, hi = part * N // parts, (part + 1) * N // parts
+                nc.vector.quantize_mx(
+                    out=codes[:, lo:hi].bitcast(FP8X4),
+                    scales=scales[:, lo:hi],
+                    in_=grouped[:, lo * PACK : hi * PACK],
+                )
+            return codes, scales
+
+        def multiply(e, slabs, group_banks, place):
+            slots = slice(e * C, (e + 1) * C)
+            for r in range(R):
+                for a, (codes, scales) in enumerate(slabs):
+                    nc.tensor.matmul_mx(
+                        out=group_banks[r][:, place, :],
+                        lhsT=codes[:, r * P : (r + 1) * P].bitcast(FP8X4),
+                        lhsT_scale=scales[:, r * P : (r + 1) * P],
+                        rhs=slot_codes[a][:, slots].bitcast(FP8X4),
+                        rhs_scale=slot_scales[4 * a : P, slots],
+                        start=(a == 0),
+                        stop=(a == PASSES - 1),
+                    )
+
+        def copy_out(first, experts, engine, group_banks):
+            for r in range(R):
+                if engine == "vector":
+                    results = y[r][:, first * C : (first + experts) * C]
+                    bias = b_sb[:, r, first : first + experts].unsqueeze(2).to_broadcast([P, experts, C])
+                    nc.vector.tensor_tensor(
+                        results.rearrange("p (e c) -> p e c", e=experts), group_banks[r][:], bias, ADD
+                    )
+                else:
+                    for i in range(experts):
+                        e = first + i
+                        nc.scalar.activation(
+                            y[r][:, e * C : (e + 1) * C],
+                            group_banks[r][:, i, :],
+                            IDENTITY,
+                            bias=b_sb[:, r, e : e + 1],
+                        )
+
+        load_x(0)
+        nc.sync.dma_start(offs_sb[:], offs)
+        load_x(1)
+        nc.sync.dma_start(out=b_sb[:], in_=b.rearrange("(p r) e -> p r e", r=R))
+
+        dst, src = interleave(x_cast[0][:], x_raw[0][:])
+        split = X_TOKENS_VECTOR // LINE
+        nc.vector.tensor_copy(out=dst[:, :split], in_=src[:, :split])
+        nc.scalar.copy(out=dst[:, split:], in_=src[:, split:])
+        dst, src = interleave(x_cast[1][:], x_raw[1][:])
+        nc.scalar.copy(out=dst, in_=src)
+        for a in range(PASSES):
+            quantise_x(a)
+        for a in range(PASSES):
+            gather_codes(a, 0)
+        gather_scales(0)
+
+        for first, experts, engine in EXPERT_GROUPS:
+            group_banks = []
+            for place in range(experts):
+                e = first + place
+                slabs = []
+                for a in range(PASSES):
+                    slab = e * PASSES + a
+                    grouped = cast_slab(slab, load_slab(slab))
+                    if slab == SLABS - 1:
+                        for i, pos in enumerate((pos1, pos2)):
+                            nc.sync.dma_start(pos_sb[i][:], pos)
+                        for i in range(2):
+                            nc.sync.dma_start(out=gate_sb[i][:], in_=gate[i, 0:P, :])
+                        nc.sync.dma_start(out=wp_raw[:], in_=wp.rearrange("(p j) f -> p j f", j=PACK))
+                    slabs.append(quantise_slab(slab, grouped))
+                    slot_piece = 1 + e
+                    if slot_piece < len(SLOT_PIECES):
+                        gather_codes(a, slot_piece)
+                        if a == PASSES - 1:
+                            gather_scales(slot_piece)
+                if place == 0:
+                    group_banks = [banks.tile([P, experts, C], F32, name="y_bank", bufs=6) for r in range(R)]
+                multiply(e, slabs, group_banks, place)
+            copy_out(first, experts, engine, group_banks)
+
+        dst, src = interleave(wp_cast[:], wp_raw[:])
+        nc.scalar.copy(out=dst, in_=src)
+        nc.vector.quantize_mx(out=wp_codes[:].bitcast(FP8X4), scales=wp_scales[:], in_=wp_cast[:])
+
+        product = [held.tile([P, R, T], F32, name=f"product{i}") for i in range(2)]
+        c_cast, c_codes, c_scales, staged = [], [], [], []
+        for k, (lo, hi) in enumerate(TOKEN_PIECES):
+            c_cast.append(held.tile([P, (hi - lo) * PACK], BF16, name=f"c_cast{k}", align_bytes=64))
+            c_codes.append(held.tile([P, hi - lo], U32, name=f"c_codes{k}", align_bytes=64))
+            c_scales.append(held.tile([P, hi - lo], U8, name=f"c_scales{k}", align_bytes=64))
+            staged.append(held.tile([P, M // P, hi - lo], F32, name=f"staged{k}"))
+
+        def gather_y(r, lo, hi):
+            for i in range(2):
+                offsets = pos_sb[i][:, lo // 16 : hi // 16]
+                nc.vector.tensor_tensor(
+                    product[i][:, r, lo:hi], y[r][:].indirect(offsets), gate_sb[i][:, lo:hi], MULT
+                )
+
+        def combine(k):
+            lo, hi = TOKEN_PIECES[k]
+            dst, first_product = interleave(c_cast[k][:], product[0][:, :, lo:hi])
+            second_product = interleave(c_cast[k][:], product[1][:, :, lo:hi])[1]
+            nc.vector.tensor_tensor(dst, first_product, second_product, ADD)
+
+        def quantise_c(k):
+            nc.vector.quantize_mx(out=c_codes[k][:].bitcast(FP8X4), scales=c_scales[k][:], in_=c_cast[k][:])
+
+        def project(k):
+            lo, hi = TOKEN_PIECES[k]
+            is_last = k == len(TOKEN_PIECES) - 1
+            for f in range(M // P):
+                acc = banks.tile([P, hi - lo], F32, name=f"out_bank{f}")
+                nc.tensor.matmul_mx(
+                    out=acc[:],
+                    lhsT=wp_codes[:, f * P : (f + 1) * P].bitcast(FP8X4),
+                    lhsT_scale=wp_scales[:, f * P : (f + 1) * P],
+                    rhs=c_codes[k][:].bitcast(FP8X4),
+                    rhs_scale=c_scales[k][:],
+                    start=True,
+                    stop=True,
+                )
+                copy = nc.vector.tensor_copy if is_last and f == 0 else nc.scalar.copy
+                copy(out=staged[k][:, f, :], in_=acc[:])
+            nc.sync.dma_start(out=out.rearrange("(f p) t -> p f t", p=P)[:, :, lo:hi], in_=staged[k][:])
+
+        for r in range(R - 1):
+            gather_y(r, 0, T)
+        token_pieces = len(TOKEN_PIECES)
+        for step in range(token_pieces + 2):
+            if step < token_pieces:
+                gather_y(R - 1, *TOKEN_PIECES[step])
+            if step >= 2:
+                project(step - 2)
+            if 1 <= step <= token_pieces:
+                quantise_c(step - 1)
+            if step < token_pieces:
+                combine(step)

@@ -1,6 +1,7 @@
 from contextlib import ExitStack
 
 import concourse.mybir as mybir
+from concourse.masks import make_identity
 
 K, T, E, C, N, M = 1024, 512, 8, 128, 512, 256
 SLOTS = E * C
@@ -27,13 +28,17 @@ LINE = 4
 SLABS = E * PASSES
 
 X_TOKENS_VECTOR = 352
-W_COLUMNS_VECTOR = [48] * (SLABS - 2) + [80] * 2
+W_COLUMNS_VECTOR = [32] * (SLABS - 2) + [64]
 
 SLOT_PIECES = [(0, 256), (256, 640), (640, 1024)]
 
-EXPERT_GROUPS = [(0, 4, "vector"), (4, 2, "vector"), (6, 2, "scalar")]
+EXPERT_GROUPS = [(0, 4, "vector", 0), (4, 2, "vector", 4), (6, 1, "scalar", 0), (7, 1, "scalar", 4)]
+BLOCKS = T // P
 
 TOKEN_PIECES = [(0, 256), (256, 384), (384, 512)]
+
+
+OUT_BANKS = [[2], [3], [4, 5]]
 
 
 def interleave(grouped, raw):
@@ -54,21 +59,26 @@ def tile_moe_nxt_lin_bias_kernel(
         code_pool = ctx.enter_context(tc.tile_pool(name="code_pool", bufs=6))
         banks = ctx.enter_context(tc.psum_pool(name="banks", bufs=1))
 
+        def bank(number, shape):
+            return banks.tile(shape, F32, name=f"bank{number}")
+
         offs_sb = held.tile([P, SLOTS // 16], U16, name="offs_sb")
         pos_sb = [held.tile([P, T // 16], U16, name=f"pos_sb{i}") for i in range(2)]
 
         x_scales = held.tile([P, T], U8, name="x_scales", align_bytes=64)
         nc.gpsimd.memset(x_scales[:], 0)
+        identity = held.tile([P, P], F32, name="identity")
+        make_identity(nc, identity[:])
+        gate_row = held.tile([P, 2, BLOCKS], F32, name="gate_row")
 
         x_raw = [held.tile([P, PACK, T], F32, name=f"x_raw{a}") for a in range(PASSES)]
         x_cast = [held.tile([P, T * PACK], BF16, name=f"x_cast{a}", align_bytes=64) for a in range(PASSES)]
         x_codes = [held.tile([P, T], U32, name=f"x_codes{a}", align_bytes=64) for a in range(PASSES)]
         slot_codes = [held.tile([P, SLOTS], U32, name=f"slot_codes{a}", align_bytes=64) for a in range(PASSES)]
         slot_scales = held.tile([P, SLOTS], U8, name="slot_scales", align_bytes=64)
-        b_sb = held.tile([P, R, E], F32, name="b_sb")
+        b_sb = held.tile([P, R, E], F32, name="b_sb", tag="bias_then_wp", align_bytes=64)
         gate_sb = [held.tile([P, T], F32, name=f"gate_sb{i}") for i in range(2)]
         wp_raw = held.tile([P, PACK, M], F32, name="wp_raw")
-        wp_cast = held.tile([P, M * PACK], BF16, name="wp_cast", align_bytes=64)
         wp_codes = held.tile([P, M], U32, name="wp_codes", align_bytes=64)
         wp_scales = held.tile([P, M], U8, name="wp_scales", align_bytes=64)
         y = [held.tile([P, SLOTS], F32, name=f"y{r}") for r in range(R)]
@@ -92,6 +102,16 @@ def tile_moe_nxt_lin_bias_kernel(
             offsets = offs_sb[:, lo // 16 : hi // 16]
             nc.vector.tensor_copy(out=slot_scales[:, lo:hi], in_=x_scales[:].indirect(offsets))
 
+        def spread_gate(i):
+            spread = bank(6 + i, [P, BLOCKS, P])
+            for m in range(BLOCKS):
+                column = gate_row[:, i, m : m + 1].to_broadcast([P, P])
+                nc.tensor.transpose(spread[:, m, :], column, identity[:])
+            nc.scalar.copy(
+                out=gate_sb[i][:].rearrange("p (q m) -> p q m", m=BLOCKS),
+                in_=spread[:].rearrange("p m q -> p q m"),
+            )
+
         def load_slab(slab):
             e, a = divmod(slab, PASSES)
             raw = slab_pool.tile([P, PACK, N], F32, name="w_raw")
@@ -103,12 +123,13 @@ def tile_moe_nxt_lin_bias_kernel(
             grouped = cast_pool.tile([P, N * PACK], BF16, name="w_cast", align_bytes=64)
             dst = grouped[:].rearrange("p (r m j) -> p m j r", r=R, j=PACK)
             src = raw[:].rearrange("p j (m r) -> p m j r", r=R)
-            split = W_COLUMNS_VECTOR[slab]
-            parts = 2 if slab == SLABS - 1 else 1
-            for copy, lo, hi in ((nc.vector.tensor_copy, 0, split), (nc.scalar.copy, split, P)):
-                for part in range(parts):
-                    rs = slice(part * R // parts, (part + 1) * R // parts)
-                    copy(out=dst[:, lo:hi, :, rs], in_=src[:, lo:hi, :, rs])
+            if slab == SLABS - 1:
+                nc.vector.tensor_copy(out=dst[:, :, :, : R // 2], in_=src[:, :, :, : R // 2])
+                nc.scalar.copy(out=dst[:, :, :, R // 2 :], in_=src[:, :, :, R // 2 :])
+            else:
+                split = W_COLUMNS_VECTOR[slab]
+                nc.vector.tensor_copy(out=dst[:, :split], in_=src[:, :split])
+                nc.scalar.copy(out=dst[:, split:], in_=src[:, split:])
             return grouped
 
         def quantise_slab(slab, grouped):
@@ -173,7 +194,7 @@ def tile_moe_nxt_lin_bias_kernel(
             gather_codes(a, 0)
         gather_scales(0)
 
-        for first, experts, engine in EXPERT_GROUPS:
+        for first, experts, engine, first_bank in EXPERT_GROUPS:
             group_banks = []
             for place in range(experts):
                 e = first + place
@@ -184,9 +205,11 @@ def tile_moe_nxt_lin_bias_kernel(
                     if slab == SLABS - 1:
                         for i, pos in enumerate((pos1, pos2)):
                             nc.sync.dma_start(pos_sb[i][:], pos)
-                        for i in range(2):
-                            nc.sync.dma_start(out=gate_sb[i][:], in_=gate[i, 0:P, :])
                         nc.sync.dma_start(out=wp_raw[:], in_=wp.rearrange("(p j) f -> p j f", j=PACK))
+                    if slab == 2:
+                        nc.sync.dma_start(out=gate_row[:], in_=gate[:, 0, :].rearrange("i (q m) -> q i m", m=BLOCKS))
+                        for i in range(2):
+                            spread_gate(i)
                     slabs.append(quantise_slab(slab, grouped))
                     slot_piece = 1 + e
                     if slot_piece < len(SLOT_PIECES):
@@ -194,65 +217,116 @@ def tile_moe_nxt_lin_bias_kernel(
                         if a == PASSES - 1:
                             gather_scales(slot_piece)
                 if place == 0:
-                    group_banks = [banks.tile([P, experts, C], F32, name="y_bank", bufs=6) for r in range(R)]
+                    group_banks = [bank(first_bank + r, [P, experts, C]) for r in range(R)]
                 multiply(e, slabs, group_banks, place)
             copy_out(first, experts, engine, group_banks)
 
+        wp_cast = held.tile([P, M * PACK], BF16, name="wp_cast", tag="bias_then_wp", align_bytes=64)
         dst, src = interleave(wp_cast[:], wp_raw[:])
         nc.scalar.copy(out=dst, in_=src)
         nc.vector.quantize_mx(out=wp_codes[:].bitcast(FP8X4), scales=wp_scales[:], in_=wp_cast[:])
 
-        product = [held.tile([P, R, T], F32, name=f"product{i}") for i in range(2)]
-        c_cast, c_codes, c_scales, staged = [], [], [], []
+        c_rows, c_cast, c_codes, c_scales, staged = [], [], [], [], []
         for k, (lo, hi) in enumerate(TOKEN_PIECES):
-            c_cast.append(held.tile([P, (hi - lo) * PACK], BF16, name=f"c_cast{k}", align_bytes=64))
+            if k < len(TOKEN_PIECES) - 1:
+                c_cast.append(held.tile([P, (hi - lo) * PACK], BF16, name=f"c_cast{k}", align_bytes=64))
             c_codes.append(held.tile([P, hi - lo], U32, name=f"c_codes{k}", align_bytes=64))
             c_scales.append(held.tile([P, hi - lo], U8, name=f"c_scales{k}", align_bytes=64))
             staged.append(held.tile([P, M // P, hi - lo], F32, name=f"staged{k}"))
+        turned_pieces = len(TOKEN_PIECES) - 1
+        last_lo = TOKEN_PIECES[-1][0]
+        for k, (lo, hi) in enumerate(TOKEN_PIECES[:turned_pieces]):
+            c_rows.append([held.tile([P, (hi - lo) // P, P, 2], BF16, name=f"c_rows{k}_{u}") for u in range(2)])
+        product = [[held.tile([P, last_lo], F32, name=f"product{r}_{i}") for i in range(2)] for r in range(R)]
 
-        def gather_y(r, lo, hi):
-            for i in range(2):
-                offsets = pos_sb[i][:, lo // 16 : hi // 16]
-                nc.vector.tensor_tensor(
-                    product[i][:, r, lo:hi], y[r][:].indirect(offsets), gate_sb[i][:, lo:hi], MULT
-                )
+        def gather_y(dst, r, i, lo, hi):
+            offsets = pos_sb[i][:, lo // 16 : hi // 16]
+            nc.vector.tensor_tensor(dst, y[r][:].indirect(offsets), gate_sb[i][:, lo:hi], MULT)
 
-        def combine(k):
+        def add_turned(r, k, sums):
             lo, hi = TOKEN_PIECES[k]
-            dst, first_product = interleave(c_cast[k][:], product[0][:, :, lo:hi])
-            second_product = interleave(c_cast[k][:], product[1][:, :, lo:hi])[1]
-            nc.vector.tensor_tensor(dst, first_product, second_product, ADD)
+            u, half = divmod(r, 2)
+            for block in range((hi - lo) // P):
+                tokens = slice(lo + block * P, lo + (block + 1) * P)
+                for i in range(2):
+                    nc.tensor.matmul(
+                        sums[:, block, half, :],
+                        lhsT=product[r][i][:, tokens],
+                        rhs=identity[:],
+                        start=(i == 0),
+                        stop=(i == 1),
+                        is_transpose=True,
+                    )
+            if half == 1:
+                nc.scalar.copy(out=c_rows[k][u][:], in_=sums[:].rearrange("t b h p -> t b p h"))
+
+        def turn_back(k):
+            lo, hi = TOKEN_PIECES[k]
+            blocks = (hi - lo) // P
+            turned = bank(k, [P, blocks, 2, P])
+            for block in range(blocks):
+                for u in range(2):
+                    pairs = c_rows[k][u][:, block].rearrange("t p h -> t (p h)").bitcast(F32)
+                    nc.tensor.transpose(turned[:, block, u, :], pairs, identity[:])
+            nc.scalar.copy(
+                out=c_cast[k][:].bitcast(F32).rearrange("p (b t u) -> p b t u", b=blocks, u=2),
+                in_=turned[:].rearrange("p b u t -> p b t u"),
+            )
 
         def quantise_c(k):
             nc.vector.quantize_mx(out=c_codes[k][:].bitcast(FP8X4), scales=c_scales[k][:], in_=c_cast[k][:])
 
         def project(k):
             lo, hi = TOKEN_PIECES[k]
-            is_last = k == len(TOKEN_PIECES) - 1
-            for f in range(M // P):
-                acc = banks.tile([P, hi - lo], F32, name=f"out_bank{f}")
-                nc.tensor.matmul_mx(
-                    out=acc[:],
-                    lhsT=wp_codes[:, f * P : (f + 1) * P].bitcast(FP8X4),
-                    lhsT_scale=wp_scales[:, f * P : (f + 1) * P],
-                    rhs=c_codes[k][:].bitcast(FP8X4),
-                    rhs_scale=c_scales[k][:],
-                    start=True,
-                    stop=True,
-                )
-                copy = nc.vector.tensor_copy if is_last and f == 0 else nc.scalar.copy
-                copy(out=staged[k][:, f, :], in_=acc[:])
+            numbers = OUT_BANKS[k]
+            per_bank = M // P // len(numbers)
+            for j, number in enumerate(numbers):
+                acc = bank(number, [P, per_bank, hi - lo])
+                for place in range(per_bank):
+                    f = j * per_bank + place
+                    nc.tensor.matmul_mx(
+                        out=acc[:, place, :],
+                        lhsT=wp_codes[:, f * P : (f + 1) * P].bitcast(FP8X4),
+                        lhsT_scale=wp_scales[:, f * P : (f + 1) * P],
+                        rhs=c_codes[k][:].bitcast(FP8X4),
+                        rhs_scale=c_scales[k][:],
+                        start=True,
+                        stop=True,
+                    )
+                copy = nc.vector.tensor_copy if j + 1 < len(numbers) else nc.scalar.copy
+                copy(out=staged[k][:, j * per_bank : (j + 1) * per_bank, :], in_=acc[:])
             nc.sync.dma_start(out=out.rearrange("(f p) t -> p f t", p=P)[:, :, lo:hi], in_=staged[k][:])
 
-        for r in range(R - 1):
-            gather_y(r, 0, T)
-        token_pieces = len(TOKEN_PIECES)
-        for step in range(token_pieces + 2):
-            if step < token_pieces:
-                gather_y(R - 1, *TOKEN_PIECES[step])
-            if step >= 2:
-                project(step - 2)
-            if 1 <= step <= token_pieces:
-                quantise_c(step - 1)
-            if step < token_pieces:
-                combine(step)
+        sums = []
+        for r in range(R):
+            u, half = divmod(r, 2)
+            if half == 0:
+                sums = [
+                    bank(4 + 2 * u + k, [P, (hi - lo) // P, 2, P])
+                    for k, (lo, hi) in enumerate(TOKEN_PIECES[:turned_pieces])
+                ]
+            if r < R - 1:
+                for i in range(2):
+                    gather_y(product[r][i][:], r, i, 0, last_lo)
+            for k, (lo, hi) in enumerate(TOKEN_PIECES[:turned_pieces]):
+                if r >= R - 1:
+                    for i in range(2):
+                        gather_y(product[r][i][:, lo:hi], r, i, lo, hi)
+                add_turned(r, k, sums[k])
+        for k in range(turned_pieces):
+            turn_back(k)
+
+        last_product = [held.tile([P, R, T - last_lo], F32, name=f"last_product{i}") for i in range(2)]
+        for r in range(R):
+            for i in range(2):
+                gather_y(last_product[i][:, r, :], r, i, last_lo, T)
+
+        quantise_c(0)
+        project(0)
+        c_cast.append(held.tile([P, (T - last_lo) * PACK], BF16, name="c_cast0", align_bytes=64))
+        dst, first_product = interleave(c_cast[-1][:], last_product[0][:])
+        second_product = interleave(c_cast[-1][:], last_product[1][:])[1]
+        nc.vector.tensor_tensor(dst, first_product, second_product, ADD)
+        for k in range(1, len(TOKEN_PIECES)):
+            quantise_c(k)
+            project(k)

@@ -28,7 +28,7 @@ LINE = 4
 SLABS = E * PASSES
 
 X_TOKENS_VECTOR = 352
-W_COLUMNS_VECTOR = [32] * (SLABS - 2) + [64]
+W_COLUMNS_VECTOR = [44] * (SLABS - 2) + [80]
 
 SLOT_PIECES = [(0, 256), (256, 640), (640, 1024)]
 
@@ -38,6 +38,7 @@ BLOCKS = T // P
 TOKEN_PIECES = [(0, 256), (256, 384), (384, 512)]
 
 
+PAIRED_EXPERTS = 5
 OUT_BANKS = [[2], [3], [4, 5]]
 
 
@@ -54,9 +55,9 @@ def tile_moe_nxt_lin_bias_kernel(
     nc = tc.nc
     with ExitStack() as ctx:
         held = ctx.enter_context(tc.tile_pool(name="held", bufs=1))
-        slab_pool = ctx.enter_context(tc.tile_pool(name="slab_pool", bufs=12))
-        cast_pool = ctx.enter_context(tc.tile_pool(name="cast_pool", bufs=4))
-        code_pool = ctx.enter_context(tc.tile_pool(name="code_pool", bufs=6))
+        slab_pool = ctx.enter_context(tc.tile_pool(name="slab_pool", bufs=4))
+        cast_pool = ctx.enter_context(tc.tile_pool(name="cast_pool", bufs=3))
+        code_pool = ctx.enter_context(tc.tile_pool(name="code_pool", bufs=4))
         banks = ctx.enter_context(tc.psum_pool(name="banks", bufs=1))
 
         def bank(number, shape):
@@ -112,17 +113,23 @@ def tile_moe_nxt_lin_bias_kernel(
                 in_=spread[:].rearrange("p m q -> p q m"),
             )
 
-        def load_slab(slab):
-            e, a = divmod(slab, PASSES)
-            raw = slab_pool.tile([P, PACK, N], F32, name="w_raw")
-            rows = w[e, a * K_PASS : (a + 1) * K_PASS, :]
-            nc.sync.dma_start(out=raw[:], in_=rows.rearrange("(p j) n -> p j n", j=PACK))
-            return raw
+        def load_expert(e):
+            if e < PAIRED_EXPERTS:
+                raw = slab_pool.tile([P, PASSES, PACK * N], F32, name="w_raw")
+                nc.sync.dma_start(out=raw[:], in_=w[e].rearrange("(a p j) n -> p a (j n)", a=PASSES, j=PACK))
+                return raw
+            slabs = []
+            for a in range(PASSES):
+                raw = slab_pool.tile([P, PACK * N], F32, name="w_raw_slab")
+                rows = w[e, a * K_PASS : (a + 1) * K_PASS, :]
+                nc.sync.dma_start(out=raw[:], in_=rows.rearrange("(p j) n -> p (j n)", j=PACK))
+                slabs.append(raw[:])
+            return slabs
 
         def cast_slab(slab, raw):
             grouped = cast_pool.tile([P, N * PACK], BF16, name="w_cast", align_bytes=64)
             dst = grouped[:].rearrange("p (r m j) -> p m j r", r=R, j=PACK)
-            src = raw[:].rearrange("p j (m r) -> p m j r", r=R)
+            src = raw.rearrange("p (j m r) -> p m j r", j=PACK, r=R)
             if slab == SLABS - 1:
                 nc.vector.tensor_copy(out=dst[:, :, :, : R // 2], in_=src[:, :, :, : R // 2])
                 nc.scalar.copy(out=dst[:, :, :, R // 2 :], in_=src[:, :, :, R // 2 :])
@@ -144,6 +151,21 @@ def tile_moe_nxt_lin_bias_kernel(
                     in_=grouped[:, lo * PACK : hi * PACK],
                 )
             return codes, scales
+
+        def cast_expert(raw):
+            grouped = cast_pool.tile([P, PASSES * N * PACK], BF16, name="w_cast_expert", align_bytes=64, bufs=2)
+            dst = grouped[:].rearrange("p (a r m j) -> p a m j r", a=PASSES, r=R, j=PACK)
+            src = raw[:].rearrange("p a (j m r) -> p a m j r", j=PACK, r=R)
+            split = W_COLUMNS_VECTOR[0]
+            nc.vector.tensor_copy(out=dst[:, :, :split], in_=src[:, :, :split])
+            nc.scalar.copy(out=dst[:, :, split:], in_=src[:, :, split:])
+            return grouped
+
+        def quantise_expert(grouped):
+            codes = code_pool.tile([P, PASSES * N], U32, name="w_codes_expert", align_bytes=64, bufs=2)
+            scales = code_pool.tile([P, PASSES * N], U8, name="w_scales_expert", align_bytes=64, bufs=2)
+            nc.vector.quantize_mx(out=codes[:].bitcast(FP8X4), scales=scales[:], in_=grouped[:])
+            return [(codes[:, a * N : (a + 1) * N], scales[:, a * N : (a + 1) * N]) for a in range(PASSES)]
 
         def multiply(e, slabs, group_banks, place):
             slots = slice(e * C, (e + 1) * C)
@@ -198,24 +220,24 @@ def tile_moe_nxt_lin_bias_kernel(
             group_banks = []
             for place in range(experts):
                 e = first + place
-                slabs = []
-                for a in range(PASSES):
-                    slab = e * PASSES + a
-                    grouped = cast_slab(slab, load_slab(slab))
-                    if slab == SLABS - 1:
-                        for i, pos in enumerate((pos1, pos2)):
-                            nc.sync.dma_start(pos_sb[i][:], pos)
-                        nc.sync.dma_start(out=wp_raw[:], in_=wp.rearrange("(p j) f -> p j f", j=PACK))
-                    if slab == 2:
-                        nc.sync.dma_start(out=gate_row[:], in_=gate[:, 0, :].rearrange("i (q m) -> q i m", m=BLOCKS))
-                        for i in range(2):
-                            spread_gate(i)
-                    slabs.append(quantise_slab(slab, grouped))
-                    slot_piece = 1 + e
-                    if slot_piece < len(SLOT_PIECES):
+                raws = load_expert(e)
+                if e == 1:
+                    nc.sync.dma_start(out=gate_row[:], in_=gate[:, 0, :].rearrange("i (q m) -> q i m", m=BLOCKS))
+                    for i in range(2):
+                        spread_gate(i)
+                if e == E - 1:
+                    for i, pos in enumerate((pos1, pos2)):
+                        nc.sync.dma_start(pos_sb[i][:], pos)
+                    nc.sync.dma_start(out=wp_raw[:], in_=wp.rearrange("(p j) f -> p j f", j=PACK))
+                if e < PAIRED_EXPERTS:
+                    slabs = quantise_expert(cast_expert(raws))
+                else:
+                    slabs = [quantise_slab(e * PASSES + a, cast_slab(e * PASSES + a, raws[a])) for a in range(PASSES)]
+                slot_piece = 1 + e
+                if slot_piece < len(SLOT_PIECES):
+                    for a in range(PASSES):
                         gather_codes(a, slot_piece)
-                        if a == PASSES - 1:
-                            gather_scales(slot_piece)
+                    gather_scales(slot_piece)
                 if place == 0:
                     group_banks = [bank(first_bank + r, [P, experts, C]) for r in range(R)]
                 multiply(e, slabs, group_banks, place)

@@ -33,7 +33,6 @@ W_COLUMNS_VECTOR = [44] * (SLABS - 2) + [80]
 SLOT_PIECES = [(0, 256), (256, 640), (640, 1024)]
 
 EXPERT_GROUPS = [(0, 4, "vector", 0), (4, 2, "vector", 4), (6, 1, "scalar", 0), (7, 1, "scalar", 4)]
-BLOCKS = T // P
 
 TOKEN_PIECES = [(0, 256), (256, 384), (384, 512)]
 
@@ -70,7 +69,6 @@ def tile_moe_nxt_lin_bias_kernel(
         nc.gpsimd.memset(x_scales[:], 0)
         identity = held.tile([P, P], F32, name="identity")
         make_identity(nc, identity[:])
-        gate_row = held.tile([P, 2, BLOCKS], F32, name="gate_row")
 
         x_raw = [held.tile([P, PACK, T], F32, name=f"x_raw{a}") for a in range(PASSES)]
         x_cast = [held.tile([P, T * PACK], BF16, name=f"x_cast{a}", align_bytes=64) for a in range(PASSES)]
@@ -102,16 +100,6 @@ def tile_moe_nxt_lin_bias_kernel(
             lo, hi = SLOT_PIECES[slot_piece]
             offsets = offs_sb[:, lo // 16 : hi // 16]
             nc.vector.tensor_copy(out=slot_scales[:, lo:hi], in_=x_scales[:].indirect(offsets))
-
-        def spread_gate(i):
-            spread = bank(6 + i, [P, BLOCKS, P])
-            for m in range(BLOCKS):
-                column = gate_row[:, i, m : m + 1].to_broadcast([P, P])
-                nc.tensor.transpose(spread[:, m, :], column, identity[:])
-            nc.scalar.copy(
-                out=gate_sb[i][:].rearrange("p (q m) -> p q m", m=BLOCKS),
-                in_=spread[:].rearrange("p m q -> p q m"),
-            )
 
         def load_expert(e):
             if e < PAIRED_EXPERTS:
@@ -221,13 +209,11 @@ def tile_moe_nxt_lin_bias_kernel(
             for place in range(experts):
                 e = first + place
                 raws = load_expert(e)
-                if e == 1:
-                    nc.sync.dma_start(out=gate_row[:], in_=gate[:, 0, :].rearrange("i (q m) -> q i m", m=BLOCKS))
-                    for i in range(2):
-                        spread_gate(i)
                 if e == E - 1:
                     for i, pos in enumerate((pos1, pos2)):
                         nc.sync.dma_start(pos_sb[i][:], pos)
+                    for i in range(2):
+                        nc.sync.dma_start(out=gate_sb[i][:], in_=gate[i, 0:P, :])
                     nc.sync.dma_start(out=wp_raw[:], in_=wp.rearrange("(p j) f -> p j f", j=PACK))
                 if e < PAIRED_EXPERTS:
                     slabs = quantise_expert(cast_expert(raws))

@@ -37,6 +37,7 @@ EXPERT_GROUPS = [(0, 4, "vector", 0), (4, 2, "vector", 4), (6, 1, "scalar", 0), 
 TOKEN_PIECES = [(0, 256), (256, 384), (384, 512)]
 
 
+LAST_FIRST_PAIR = [(0, 44, 64), (64, 108, 128)]
 PAIRED_EXPERTS = 5
 OUT_BANKS = [[2], [3], [4, 5]]
 
@@ -78,9 +79,8 @@ def tile_moe_nxt_lin_bias_kernel(
         b_sb = held.tile([P, R, E], F32, name="b_sb", tag="bias_then_wp", align_bytes=64)
         gate_sb = [held.tile([P, T], F32, name=f"gate_sb{i}") for i in range(2)]
         wp_raw = held.tile([P, PACK, M], F32, name="wp_raw")
-        wp_codes = held.tile([P, M], U32, name="wp_codes", align_bytes=64)
         wp_scales = held.tile([P, M], U8, name="wp_scales", align_bytes=64)
-        y = [held.tile([P, SLOTS], F32, name=f"y{r}") for r in range(R)]
+        y = [held.tile([P, SLOTS], F32, name=f"y{r}", align_bytes=64) for r in range(R)]
 
         def load_x(a):
             rows = xT[a * K_PASS : (a + 1) * K_PASS, :]
@@ -110,7 +110,13 @@ def tile_moe_nxt_lin_bias_kernel(
             for a in range(PASSES):
                 raw = slab_pool.tile([P, PACK * N], F32, name="w_raw_slab")
                 rows = w[e, a * K_PASS : (a + 1) * K_PASS, :]
-                nc.sync.dma_start(out=raw[:], in_=rows.rearrange("(p j) n -> p (j n)", j=PACK))
+                rows = rows.rearrange("(p j) n -> p (j n)", j=PACK)
+                if e * PASSES + a == SLABS - 1:
+                    cut = PACK * N - N // 2
+                    nc.sync.dma_start(out=raw[:, :cut], in_=rows[:, :cut])
+                    nc.sync.dma_start(out=raw[:, cut:], in_=rows[:, cut:])
+                else:
+                    nc.sync.dma_start(out=raw[:], in_=rows)
                 slabs.append(raw[:])
             return slabs
 
@@ -119,8 +125,10 @@ def tile_moe_nxt_lin_bias_kernel(
             dst = grouped[:].rearrange("p (r m j) -> p m j r", r=R, j=PACK)
             src = raw.rearrange("p (j m r) -> p m j r", j=PACK, r=R)
             if slab == SLABS - 1:
-                nc.vector.tensor_copy(out=dst[:, :, :, : R // 2], in_=src[:, :, :, : R // 2])
-                nc.scalar.copy(out=dst[:, :, :, R // 2 :], in_=src[:, :, :, R // 2 :])
+                for lo, mid, hi in LAST_FIRST_PAIR:
+                    nc.vector.tensor_copy(out=dst[:, lo:mid, :, :2], in_=src[:, lo:mid, :, :2])
+                    nc.scalar.copy(out=dst[:, mid:hi, :, :2], in_=src[:, mid:hi, :, :2])
+                nc.scalar.copy(out=dst[:, :, :, 2:], in_=src[:, :, :, 2:])
             else:
                 split = W_COLUMNS_VECTOR[slab]
                 nc.vector.tensor_copy(out=dst[:, :split], in_=src[:, :split])
@@ -232,7 +240,6 @@ def tile_moe_nxt_lin_bias_kernel(
         wp_cast = held.tile([P, M * PACK], BF16, name="wp_cast", tag="bias_then_wp", align_bytes=64)
         dst, src = interleave(wp_cast[:], wp_raw[:])
         nc.scalar.copy(out=dst, in_=src)
-        nc.vector.quantize_mx(out=wp_codes[:].bitcast(FP8X4), scales=wp_scales[:], in_=wp_cast[:])
 
         c_rows, c_cast, c_codes, c_scales, staged = [], [], [], [], []
         for k, (lo, hi) in enumerate(TOKEN_PIECES):
@@ -329,6 +336,8 @@ def tile_moe_nxt_lin_bias_kernel(
             for i in range(2):
                 gather_y(last_product[i][:, r, :], r, i, last_lo, T)
 
+        wp_codes = held.tile([P, M], U32, name="y1", align_bytes=64)
+        nc.vector.quantize_mx(out=wp_codes[:].bitcast(FP8X4), scales=wp_scales[:], in_=wp_cast[:])
         quantise_c(0)
         project(0)
         c_cast.append(held.tile([P, (T - last_lo) * PACK], BF16, name="c_cast0", align_bytes=64))

@@ -39,7 +39,7 @@ TOKEN_PIECES = [(0, 256), (256, 384), (384, 512)]
 
 LAST_FIRST_PAIR = [(0, 44, 64), (64, 108, 128)]
 PAIRED_EXPERTS = 5
-OUT_BANKS = [[2], [3], [4, 5]]
+OUT_BANKS = [[2, 3], [6], [4, 5]]
 
 
 def interleave(grouped, raw):
@@ -308,9 +308,12 @@ def tile_moe_nxt_lin_bias_kernel(
                         start=True,
                         stop=True,
                     )
-                copy = nc.vector.tensor_copy if j + 1 < len(numbers) else nc.scalar.copy
+                copy = nc.vector.tensor_copy if k == len(TOKEN_PIECES) - 1 else nc.scalar.copy
                 copy(out=staged[k][:, j * per_bank : (j + 1) * per_bank, :], in_=acc[:])
-            nc.sync.dma_start(out=out.rearrange("(f p) t -> p f t", p=P)[:, :, lo:hi], in_=staged[k][:])
+                if len(numbers) > 1:
+                    nc.sync.dma_start(out=out[j * P : (j + 1) * P, lo:hi], in_=staged[k][:, j, :])
+            if len(numbers) == 1:
+                nc.sync.dma_start(out=out.rearrange("(f p) t -> p f t", p=P)[:, :, lo:hi], in_=staged[k][:])
 
         sums = []
         for r in range(R):

@@ -39,7 +39,7 @@ TOKEN_PIECES = [(0, 256), (256, 384), (384, 512)]
 
 LAST_FIRST_PAIR = [(0, 44, 64), (64, 108, 128)]
 PAIRED_EXPERTS = 5
-OUT_BANKS = [[2, 3], [6], [4, 5]]
+OUT_BANKS = [[2, 3], [7], [6, 0], [4, 5]]
 
 
 def interleave(grouped, raw):
@@ -241,13 +241,10 @@ def tile_moe_nxt_lin_bias_kernel(
         dst, src = interleave(wp_cast[:], wp_raw[:])
         nc.scalar.copy(out=dst, in_=src)
 
-        c_rows, c_cast, c_codes, c_scales, staged = [], [], [], [], []
+        c_rows, c_cast = [], []
         for k, (lo, hi) in enumerate(TOKEN_PIECES):
             if k < len(TOKEN_PIECES) - 1:
                 c_cast.append(held.tile([P, (hi - lo) * PACK], BF16, name=f"c_cast{k}", align_bytes=64))
-            c_codes.append(held.tile([P, hi - lo], U32, name=f"c_codes{k}", align_bytes=64))
-            c_scales.append(held.tile([P, hi - lo], U8, name=f"c_scales{k}", align_bytes=64))
-            staged.append(held.tile([P, M // P, hi - lo], F32, name=f"staged{k}"))
         turned_pieces = len(TOKEN_PIECES) - 1
         last_lo = TOKEN_PIECES[-1][0]
         for k, (lo, hi) in enumerate(TOKEN_PIECES[:turned_pieces]):
@@ -288,32 +285,33 @@ def tile_moe_nxt_lin_bias_kernel(
                 in_=turned[:].rearrange("p b u t -> p b t u"),
             )
 
-        def quantise_c(k):
-            nc.vector.quantize_mx(out=c_codes[k][:].bitcast(FP8X4), scales=c_scales[k][:], in_=c_cast[k][:])
-
-        def project(k):
-            lo, hi = TOKEN_PIECES[k]
-            numbers = OUT_BANKS[k]
+        def project(block, grouped):
+            codes = held.tile([P, P], U32, name=f"c_codes{block}", align_bytes=64)
+            scales = held.tile([P, P], U8, name=f"c_scales{block}", align_bytes=64)
+            nc.vector.quantize_mx(out=codes[:].bitcast(FP8X4), scales=scales[:], in_=grouped)
+            staged = held.tile([P, M // P, P], F32, name=f"staged{block}")
+            tokens = slice(block * P, (block + 1) * P)
+            numbers = OUT_BANKS[block]
             per_bank = M // P // len(numbers)
             for j, number in enumerate(numbers):
-                acc = bank(number, [P, per_bank, hi - lo])
+                acc = bank(number, [P, per_bank, P])
                 for place in range(per_bank):
                     f = j * per_bank + place
                     nc.tensor.matmul_mx(
                         out=acc[:, place, :],
                         lhsT=wp_codes[:, f * P : (f + 1) * P].bitcast(FP8X4),
                         lhsT_scale=wp_scales[:, f * P : (f + 1) * P],
-                        rhs=c_codes[k][:].bitcast(FP8X4),
-                        rhs_scale=c_scales[k][:],
+                        rhs=codes[:].bitcast(FP8X4),
+                        rhs_scale=scales[:],
                         start=True,
                         stop=True,
                     )
-                copy = nc.vector.tensor_copy if k == len(TOKEN_PIECES) - 1 else nc.scalar.copy
-                copy(out=staged[k][:, j * per_bank : (j + 1) * per_bank, :], in_=acc[:])
+                copy = nc.vector.tensor_copy if block == len(OUT_BANKS) - 1 else nc.scalar.copy
+                copy(out=staged[:, j * per_bank : (j + 1) * per_bank, :], in_=acc[:])
                 if len(numbers) > 1:
-                    nc.sync.dma_start(out=out[j * P : (j + 1) * P, lo:hi], in_=staged[k][:, j, :])
+                    nc.sync.dma_start(out=out[j * P : (j + 1) * P, tokens], in_=staged[:, j, :])
             if len(numbers) == 1:
-                nc.sync.dma_start(out=out.rearrange("(f p) t -> p f t", p=P)[:, :, lo:hi], in_=staged[k][:])
+                nc.sync.dma_start(out=out.rearrange("(f p) t -> p f t", p=P)[:, :, tokens], in_=staged[:])
 
         sums = []
         for r in range(R):
@@ -341,12 +339,11 @@ def tile_moe_nxt_lin_bias_kernel(
 
         wp_codes = held.tile([P, M], U32, name="y1", align_bytes=64)
         nc.vector.quantize_mx(out=wp_codes[:].bitcast(FP8X4), scales=wp_scales[:], in_=wp_cast[:])
-        quantise_c(0)
-        project(0)
-        c_cast.append(held.tile([P, (T - last_lo) * PACK], BF16, name="c_cast0", align_bytes=64))
-        dst, first_product = interleave(c_cast[-1][:], last_product[0][:])
-        second_product = interleave(c_cast[-1][:], last_product[1][:])[1]
+        for block in range(2):
+            project(block, c_cast[0][:, block * P * PACK : (block + 1) * P * PACK])
+        c_cast.append(c_cast[0][:, : (T - last_lo) * PACK])
+        dst, first_product = interleave(c_cast[-1], last_product[0][:])
+        second_product = interleave(c_cast[-1], last_product[1][:])[1]
         nc.vector.tensor_tensor(dst, first_product, second_product, ADD)
-        for k in range(1, len(TOKEN_PIECES)):
-            quantise_c(k)
-            project(k)
+        project(2, c_cast[1][:])
+        project(3, c_cast[2])

@@ -18,6 +18,7 @@ FP8X4 = mybir.dt.float8_e4m3fn_x4
 MULT = mybir.AluOpType.mult
 ADD = mybir.AluOpType.add
 IDENTITY = mybir.ActivationFunctionType.Identity
+COPY = mybir.ActivationFunctionType.Copy
 
 P = 128
 PACK = 4
@@ -34,12 +35,13 @@ SLOT_PIECES = [(0, 256), (256, 640), (640, 1024)]
 
 EXPERT_GROUPS = [(0, 4, "vector", 0), (4, 2, "vector", 4), (6, 1, "scalar", 0), (7, 1, "scalar", 4)]
 
-TOKEN_PIECES = [(0, 256), (256, 384), (384, 512)]
+TURNED_PIECES = [(0, 256), (256, 384)]
+TURNED = TURNED_PIECES[-1][1]
 
 
 LAST_FIRST_PAIR = [(0, 44, 64), (64, 108, 128)]
 PAIRED_EXPERTS = 5
-OUT_BANKS = [[2, 3], [7], [6, 0], [4, 5]]
+OUT_BANKS = [[0], [1, 2], [3, 7], [3, 7]]
 
 
 def interleave(grouped, raw):
@@ -77,7 +79,9 @@ def tile_moe_nxt_lin_bias_kernel(
         slot_codes = [held.tile([P, SLOTS], U32, name=f"slot_codes{a}", align_bytes=64) for a in range(PASSES)]
         slot_scales = held.tile([P, SLOTS], U8, name="slot_scales", align_bytes=64)
         b_sb = held.tile([P, R, E], F32, name="b_sb", tag="bias_then_wp", align_bytes=64)
-        gate_sb = [held.tile([P, T], F32, name=f"gate_sb{i}") for i in range(2)]
+        first_gate = held.tile([P, T], F32, name="first_gate")
+        last_gate = held.tile([P, T - TURNED], F32, name="last_gate")
+        turned_gate = held.tile([P, TURNED // P, 8], F32, name="turned_gate")
         wp_raw = held.tile([P, PACK, M], F32, name="wp_raw")
         wp_scales = held.tile([P, M], U8, name="wp_scales", align_bytes=64)
         y = [held.tile([P, SLOTS], F32, name=f"y{r}", align_bytes=64) for r in range(R)]
@@ -220,9 +224,13 @@ def tile_moe_nxt_lin_bias_kernel(
                 if e == E - 1:
                     for i, pos in enumerate((pos1, pos2)):
                         nc.sync.dma_start(pos_sb[i][:], pos)
-                    for i in range(2):
-                        nc.sync.dma_start(out=gate_sb[i][:], in_=gate[i, 0:P, :])
+                    nc.sync.dma_start(out=first_gate[:], in_=gate[0, 0:P, :])
                     nc.sync.dma_start(out=wp_raw[:], in_=wp.rearrange("(p j) f -> p j f", j=PACK))
+                    with nc.allow_non_contiguous_dma(reason="one gate value a partition"):
+                        nc.sync.dma_start(
+                            out=turned_gate[:, :, 0], in_=gate[1, 0, 0:TURNED].rearrange("(b t) -> t b", t=P)
+                        )
+                    nc.sync.dma_start(out=last_gate[:], in_=gate[1, 0:P, TURNED:])
                 if e < PAIRED_EXPERTS:
                     slabs = quantise_expert(cast_expert(raws))
                 else:
@@ -238,54 +246,12 @@ def tile_moe_nxt_lin_bias_kernel(
             copy_out(first, experts, engine, group_banks)
 
         wp_cast = held.tile([P, M * PACK], BF16, name="wp_cast", tag="bias_then_wp", align_bytes=64)
-        dst, src = interleave(wp_cast[:], wp_raw[:])
-        nc.scalar.copy(out=dst, in_=src)
+        wp_codes = held.tile([P, M], U32, name="wp_codes", align_bytes=64)
 
-        c_rows, c_cast = [], []
-        for k, (lo, hi) in enumerate(TOKEN_PIECES):
-            if k < len(TOKEN_PIECES) - 1:
-                c_cast.append(held.tile([P, (hi - lo) * PACK], BF16, name=f"c_cast{k}", align_bytes=64))
-        turned_pieces = len(TOKEN_PIECES) - 1
-        last_lo = TOKEN_PIECES[-1][0]
-        for k, (lo, hi) in enumerate(TOKEN_PIECES[:turned_pieces]):
-            c_rows.append([held.tile([P, (hi - lo) // P, P, 2], BF16, name=f"c_rows{k}_{u}") for u in range(2)])
-        product = [[held.tile([P, last_lo], F32, name=f"product{r}_{i}") for i in range(2)] for r in range(R)]
+        def offsets_of(i, lo, hi):
+            return pos_sb[i][:, lo // 16 : hi // 16]
 
-        def gather_y(dst, r, i, lo, hi):
-            offsets = pos_sb[i][:, lo // 16 : hi // 16]
-            nc.vector.tensor_tensor(dst, y[r][:].indirect(offsets), gate_sb[i][:, lo:hi], MULT)
-
-        def add_turned(r, k, sums):
-            lo, hi = TOKEN_PIECES[k]
-            u, half = divmod(r, 2)
-            for block in range((hi - lo) // P):
-                tokens = slice(lo + block * P, lo + (block + 1) * P)
-                for i in range(2):
-                    nc.tensor.matmul(
-                        sums[:, block, half, :],
-                        lhsT=product[r][i][:, tokens],
-                        rhs=identity[:],
-                        start=(i == 0),
-                        stop=(i == 1),
-                        is_transpose=True,
-                    )
-            if half == 1:
-                nc.scalar.copy(out=c_rows[k][u][:], in_=sums[:].rearrange("t b h p -> t b p h"))
-
-        def turn_back(k):
-            lo, hi = TOKEN_PIECES[k]
-            blocks = (hi - lo) // P
-            turned = bank(k, [P, blocks, 2, P])
-            for block in range(blocks):
-                for u in range(2):
-                    pairs = c_rows[k][u][:, block].rearrange("t p h -> t (p h)").bitcast(F32)
-                    nc.tensor.transpose(turned[:, block, u, :], pairs, identity[:])
-            nc.scalar.copy(
-                out=c_cast[k][:].bitcast(F32).rearrange("p (b t u) -> p b t u", b=blocks, u=2),
-                in_=turned[:].rearrange("p b u t -> p b t u"),
-            )
-
-        def project(block, grouped):
+        def project(block, grouped, copy):
             codes = held.tile([P, P], U32, name=f"c_codes{block}", align_bytes=64)
             scales = held.tile([P, P], U8, name=f"c_scales{block}", align_bytes=64)
             nc.vector.quantize_mx(out=codes[:].bitcast(FP8X4), scales=scales[:], in_=grouped)
@@ -306,44 +272,56 @@ def tile_moe_nxt_lin_bias_kernel(
                         start=True,
                         stop=True,
                     )
-                copy = nc.vector.tensor_copy if block == len(OUT_BANKS) - 1 else nc.scalar.copy
                 copy(out=staged[:, j * per_bank : (j + 1) * per_bank, :], in_=acc[:])
                 if len(numbers) > 1:
                     nc.sync.dma_start(out=out[j * P : (j + 1) * P, tokens], in_=staged[:, j, :])
             if len(numbers) == 1:
                 nc.sync.dma_start(out=out.rearrange("(f p) t -> p f t", p=P)[:, :, tokens], in_=staged[:])
 
-        sums = []
-        for r in range(R):
-            u, half = divmod(r, 2)
-            if half == 0:
-                sums = [
-                    bank(4 + 2 * u + k, [P, (hi - lo) // P, 2, P])
-                    for k, (lo, hi) in enumerate(TOKEN_PIECES[:turned_pieces])
-                ]
-            if r < R - 1:
-                for i in range(2):
-                    gather_y(product[r][i][:], r, i, 0, last_lo)
-            for k, (lo, hi) in enumerate(TOKEN_PIECES[:turned_pieces]):
-                if r >= R - 1:
-                    for i in range(2):
-                        gather_y(product[r][i][:, lo:hi], r, i, lo, hi)
-                add_turned(r, k, sums[k])
-        for k in range(turned_pieces):
-            turn_back(k)
+        def add_rounded(block, first, second):
+            grouped = held.tile([P, P * PACK], BF16, name=f"c_cast{block}", align_bytes=64)
+            dst, first = interleave(grouped[:], first)
+            nc.vector.tensor_tensor(dst, first, interleave(grouped[:], second)[1], ADD)
+            return grouped
 
-        last_product = [held.tile([P, R, T - last_lo], F32, name=f"last_product{i}") for i in range(2)]
+        first_product = held.tile([P, R, T], F32, name="first_product", tag="x_raw0")
         for r in range(R):
-            for i in range(2):
-                gather_y(last_product[i][:, r, :], r, i, last_lo, T)
+            nc.vector.tensor_tensor(
+                first_product[:, r, :], y[r][:].indirect(offsets_of(0, 0, T)), first_gate[:], MULT
+            )
+        last_product = held.tile([P, R, T - TURNED], F32, name="last_product")
+        for r in range(R):
+            nc.vector.tensor_tensor(
+                last_product[:, r, :], y[r][:].indirect(offsets_of(1, TURNED, T)), last_gate[:], MULT
+            )
 
-        wp_codes = held.tile([P, M], U32, name="y1", align_bytes=64)
+        turned = []
+        for k, (lo, hi) in enumerate(TURNED_PIECES):
+            plain = held.tile([P, R, hi - lo], F32, name=f"plain{k}")
+            blocks = range(lo // P, hi // P)
+            for block in blocks:
+                turned.append(bank(block, [P, R, P]))
+            for r in range(R):
+                nc.scalar.activation(plain[:, r, :], y[r][:].indirect(offsets_of(1, lo, hi)), COPY)
+                for block in blocks:
+                    tokens = slice(block * P - lo, (block + 1) * P - lo)
+                    nc.tensor.transpose(turned[block][:, r, :], plain[:, r, tokens], identity[:])
+        second_product = []
+        for block in range(TURNED // P):
+            scaled = held.tile([P, R, P], F32, name=f"scaled{block}")
+            nc.scalar.activation(scaled[:], turned[block][:], COPY, scale=turned_gate[:, block, 0:1])
+            back = bank(4 + block, [P, R, P])
+            for r in range(R):
+                nc.tensor.transpose(back[:, r, :], scaled[:, r, :], identity[:])
+            second_product.append(back)
+
+        dst, src = interleave(wp_cast[:], wp_raw[:])
+        nc.scalar.copy(out=dst, in_=src)
         nc.vector.quantize_mx(out=wp_codes[:].bitcast(FP8X4), scales=wp_scales[:], in_=wp_cast[:])
-        for block in range(2):
-            project(block, c_cast[0][:, block * P * PACK : (block + 1) * P * PACK])
-        c_cast.append(c_cast[0][:, : (T - last_lo) * PACK])
-        dst, first_product = interleave(c_cast[-1], last_product[0][:])
-        second_product = interleave(c_cast[-1], last_product[1][:])[1]
-        nc.vector.tensor_tensor(dst, first_product, second_product, ADD)
-        project(2, c_cast[1][:])
-        project(3, c_cast[2])
+
+        last_block = T // P - 1
+        grouped = add_rounded(last_block, last_product[:], first_product[:, :, TURNED:])
+        project(last_block, grouped[:], nc.scalar.copy)
+        for block in range(TURNED // P):
+            grouped = add_rounded(block, second_product[block][:], first_product[:, :, block * P : (block + 1) * P])
+            project(block, grouped[:], nc.vector.tensor_copy if block == TURNED // P - 1 else nc.scalar.copy)

@@ -78,7 +78,7 @@ def tile_moe_nxt_lin_bias_kernel(
         x_codes = [held.tile([P, T], U32, name=f"x_codes{a}", align_bytes=64) for a in range(PASSES)]
         slot_codes = [held.tile([P, SLOTS], U32, name=f"slot_codes{a}", align_bytes=64) for a in range(PASSES)]
         slot_scales = held.tile([P, SLOTS], U8, name="slot_scales", align_bytes=64)
-        b_sb = held.tile([P, R, E], F32, name="b_sb", tag="bias_then_wp", align_bytes=64)
+        b_sb = held.tile([P, R, E], F32, name="b_sb")
         first_gate = held.tile([P, T], F32, name="first_gate")
         last_gate = held.tile([P, T - TURNED], F32, name="last_gate")
         turned_gate = held.tile([P, TURNED // P, 8], F32, name="turned_gate")
@@ -225,12 +225,12 @@ def tile_moe_nxt_lin_bias_kernel(
                     for i, pos in enumerate((pos1, pos2)):
                         nc.sync.dma_start(pos_sb[i][:], pos)
                     nc.sync.dma_start(out=first_gate[:], in_=gate[0, 0:P, :])
-                    nc.sync.dma_start(out=wp_raw[:], in_=wp.rearrange("(p j) f -> p j f", j=PACK))
                     with nc.allow_non_contiguous_dma(reason="one gate value a partition"):
                         nc.sync.dma_start(
                             out=turned_gate[:, :, 0], in_=gate[1, 0, 0:TURNED].rearrange("(b t) -> t b", t=P)
                         )
                     nc.sync.dma_start(out=last_gate[:], in_=gate[1, 0:P, TURNED:])
+                    nc.sync.dma_start(out=wp_raw[:], in_=wp.rearrange("(p j) f -> p j f", j=PACK))
                 if e < PAIRED_EXPERTS:
                     slabs = quantise_expert(cast_expert(raws))
                 else:
@@ -245,14 +245,13 @@ def tile_moe_nxt_lin_bias_kernel(
                 multiply(e, slabs, group_banks, place)
             copy_out(first, experts, engine, group_banks)
 
-        wp_cast = held.tile([P, M * PACK], BF16, name="wp_cast", tag="bias_then_wp", align_bytes=64)
         wp_codes = held.tile([P, M], U32, name="wp_codes", align_bytes=64)
 
         def offsets_of(i, lo, hi):
             return pos_sb[i][:, lo // 16 : hi // 16]
 
-        def project(block, grouped, copy):
-            codes = held.tile([P, P], U32, name=f"c_codes{block}", align_bytes=64)
+        def project(block, grouped, place_of_codes, copy):
+            codes = held.tile([P, P], U32, name=f"c_codes{block}", tag=place_of_codes, align_bytes=64)
             scales = held.tile([P, P], U8, name=f"c_scales{block}", align_bytes=64)
             nc.vector.quantize_mx(out=codes[:].bitcast(FP8X4), scales=scales[:], in_=grouped)
             staged = held.tile([P, M // P, P], F32, name=f"staged{block}")
@@ -272,7 +271,7 @@ def tile_moe_nxt_lin_bias_kernel(
                         start=True,
                         stop=True,
                     )
-                copy(out=staged[:, j * per_bank : (j + 1) * per_bank, :], in_=acc[:])
+                copy[j](out=staged[:, j * per_bank : (j + 1) * per_bank, :], in_=acc[:])
                 if len(numbers) > 1:
                     nc.sync.dma_start(out=out[j * P : (j + 1) * P, tokens], in_=staged[:, j, :])
             if len(numbers) == 1:
@@ -297,7 +296,7 @@ def tile_moe_nxt_lin_bias_kernel(
 
         turned = []
         for k, (lo, hi) in enumerate(TURNED_PIECES):
-            plain = held.tile([P, R, hi - lo], F32, name=f"plain{k}")
+            plain = held.tile([P, R, hi - lo], F32, name=f"plain{k}", align_bytes=64)
             blocks = range(lo // P, hi // P)
             for block in blocks:
                 turned.append(bank(block, [P, R, P]))
@@ -308,20 +307,23 @@ def tile_moe_nxt_lin_bias_kernel(
                     nc.tensor.transpose(turned[block][:, r, :], plain[:, r, tokens], identity[:])
         second_product = []
         for block in range(TURNED // P):
-            scaled = held.tile([P, R, P], F32, name=f"scaled{block}")
+            if block == TURNED // P - 1:
+                wp_cast = held.tile([P, M * PACK], BF16, name="wp_cast", tag="plain0", align_bytes=64)
+                dst, src = interleave(wp_cast[:], wp_raw[:])
+                nc.scalar.copy(out=dst, in_=src)
+                nc.vector.quantize_mx(out=wp_codes[:].bitcast(FP8X4), scales=wp_scales[:], in_=wp_cast[:])
+            scaled = held.tile([P, R, P], F32, name=f"scaled{block}", align_bytes=64)
             nc.scalar.activation(scaled[:], turned[block][:], COPY, scale=turned_gate[:, block, 0:1])
             back = bank(4 + block, [P, R, P])
             for r in range(R):
                 nc.tensor.transpose(back[:, r, :], scaled[:, r, :], identity[:])
             second_product.append(back)
 
-        dst, src = interleave(wp_cast[:], wp_raw[:])
-        nc.scalar.copy(out=dst, in_=src)
-        nc.vector.quantize_mx(out=wp_codes[:].bitcast(FP8X4), scales=wp_scales[:], in_=wp_cast[:])
 
         last_block = T // P - 1
-        grouped = add_rounded(last_block, last_product[:], first_product[:, :, TURNED:])
-        project(last_block, grouped[:], nc.scalar.copy)
+        waiting = (last_block, add_rounded(last_block, last_product[:], first_product[:, :, TURNED:]))
         for block in range(TURNED // P):
             grouped = add_rounded(block, second_product[block][:], first_product[:, :, block * P : (block + 1) * P])
-            project(block, grouped[:], nc.vector.tensor_copy if block == TURNED // P - 1 else nc.scalar.copy)
+            project(waiting[0], waiting[1][:], f"scaled{block}", [nc.scalar.copy] * 2)
+            waiting = (block, grouped)
+        project(waiting[0], waiting[1][:], "last_codes", [nc.vector.tensor_copy, nc.scalar.copy])

@@ -40,14 +40,15 @@ TURNED = TURNED_PIECES[-1][1]
 
 
 LAST_FIRST_PAIR = [(0, 44, 64), (64, 108, 128)]
+LAST_SECOND_PAIR = 80
 PAIRED_EXPERTS = 5
-OUT_BANKS = [[0], [1, 2], [3, 7], [3, 7]]
+OUT_BANKS = [[0], [1, 3], [7, 4], [2]]
 
 
-def interleave(grouped, raw):
+def interleave(grouped, raw, run=LINE):
     return (
-        grouped.rearrange("p (c i j) -> p c j i", i=LINE, j=PACK),
-        raw.rearrange("p j (c i) -> p c j i", i=LINE),
+        grouped.rearrange("p (c i j) -> p c j i", i=run, j=PACK),
+        raw.rearrange("p j (c i) -> p c j i", i=run),
     )
 
 
@@ -89,6 +90,12 @@ def tile_moe_nxt_lin_bias_kernel(
         def load_x(a):
             rows = xT[a * K_PASS : (a + 1) * K_PASS, :]
             nc.sync.dma_start(out=x_raw[a][:], in_=rows.rearrange("(p j) t -> p j t", j=PACK))
+
+        def load_turned_gate(lo, hi):
+            with nc.allow_non_contiguous_dma(reason="one gate value a partition"):
+                nc.sync.dma_start(
+                    out=turned_gate[:, lo:hi, 0], in_=gate[1, 0, lo * P : hi * P].rearrange("(b t) -> t b", t=P)
+                )
 
         def quantise_x(a):
             nc.vector.quantize_mx(
@@ -132,7 +139,8 @@ def tile_moe_nxt_lin_bias_kernel(
                 for lo, mid, hi in LAST_FIRST_PAIR:
                     nc.vector.tensor_copy(out=dst[:, lo:mid, :, :2], in_=src[:, lo:mid, :, :2])
                     nc.scalar.copy(out=dst[:, mid:hi, :, :2], in_=src[:, mid:hi, :, :2])
-                nc.scalar.copy(out=dst[:, :, :, 2:], in_=src[:, :, :, 2:])
+                nc.vector.tensor_copy(out=dst[:, LAST_SECOND_PAIR:, :, 2:], in_=src[:, LAST_SECOND_PAIR:, :, 2:])
+                nc.scalar.copy(out=dst[:, :LAST_SECOND_PAIR, :, 2:], in_=src[:, :LAST_SECOND_PAIR, :, 2:])
             else:
                 split = W_COLUMNS_VECTOR[slab]
                 nc.vector.tensor_copy(out=dst[:, :split], in_=src[:, :split])
@@ -225,12 +233,10 @@ def tile_moe_nxt_lin_bias_kernel(
                     for i, pos in enumerate((pos1, pos2)):
                         nc.sync.dma_start(pos_sb[i][:], pos)
                     nc.sync.dma_start(out=first_gate[:], in_=gate[0, 0:P, :])
-                    with nc.allow_non_contiguous_dma(reason="one gate value a partition"):
-                        nc.sync.dma_start(
-                            out=turned_gate[:, :, 0], in_=gate[1, 0, 0:TURNED].rearrange("(b t) -> t b", t=P)
-                        )
+                    load_turned_gate(0, 1)
                     nc.sync.dma_start(out=last_gate[:], in_=gate[1, 0:P, TURNED:])
                     nc.sync.dma_start(out=wp_raw[:], in_=wp.rearrange("(p j) f -> p j f", j=PACK))
+                    load_turned_gate(1, TURNED // P)
                 if e < PAIRED_EXPERTS:
                     slabs = quantise_expert(cast_expert(raws))
                 else:
@@ -279,8 +285,8 @@ def tile_moe_nxt_lin_bias_kernel(
 
         def add_rounded(block, first, second):
             grouped = held.tile([P, P * PACK], BF16, name=f"c_cast{block}", align_bytes=64)
-            dst, first = interleave(grouped[:], first)
-            nc.vector.tensor_tensor(dst, first, interleave(grouped[:], second)[1], ADD)
+            dst, first = interleave(grouped[:], first, run=2)
+            nc.vector.tensor_tensor(dst, first, interleave(grouped[:], second, run=2)[1], ADD)
             return grouped
 
         first_product = held.tile([P, R, T], F32, name="first_product", tag="x_raw0")
@@ -307,7 +313,7 @@ def tile_moe_nxt_lin_bias_kernel(
                     nc.tensor.transpose(turned[block][:, r, :], plain[:, r, tokens], identity[:])
         second_product = []
         for block in range(TURNED // P):
-            if block == TURNED // P - 1:
+            if block == 1:
                 wp_cast = held.tile([P, M * PACK], BF16, name="wp_cast", tag="plain0", align_bytes=64)
                 dst, src = interleave(wp_cast[:], wp_raw[:])
                 nc.scalar.copy(out=dst, in_=src)
@@ -324,6 +330,6 @@ def tile_moe_nxt_lin_bias_kernel(
         waiting = (last_block, add_rounded(last_block, last_product[:], first_product[:, :, TURNED:]))
         for block in range(TURNED // P):
             grouped = add_rounded(block, second_product[block][:], first_product[:, :, block * P : (block + 1) * P])
-            project(waiting[0], waiting[1][:], f"scaled{block}", [nc.scalar.copy] * 2)
+            project(waiting[0], waiting[1][:], f"scaled{block}" if block else "first_codes", [nc.scalar.copy] * 2)
             waiting = (block, grouped)
         project(waiting[0], waiting[1][:], "last_codes", [nc.vector.tensor_copy, nc.scalar.copy])

@@ -29,7 +29,7 @@ LINE = 4
 SLABS = E * PASSES
 
 X_TOKENS_VECTOR = 352
-W_COLUMNS_VECTOR = [44] * (SLABS - 2) + [80]
+W_COLUMNS_VECTOR = [44] * (SLABS - 2) + [64]
 
 SLOT_PIECES = [(0, 256), (256, 640), (640, 1024)]
 
@@ -39,8 +39,8 @@ TURNED_PIECES = [(0, 256), (256, 384)]
 TURNED = TURNED_PIECES[-1][1]
 
 
-LAST_FIRST_PAIR = [(0, 44, 64), (64, 108, 128)]
-LAST_SECOND_PAIR = 80
+LAST_FIRST_PAIR = [(0, 36, 64), (64, 100, 128)]
+LAST_SECOND_PAIR = 88
 PAIRED_EXPERTS = 5
 OUT_BANKS = [[0], [1, 3], [7, 4], [2]]
 

@@ -39,8 +39,8 @@ TURNED_PIECES = [(0, 256), (256, 384)]
 TURNED = TURNED_PIECES[-1][1]
 
 
-LAST_FIRST_PAIR = [(0, 36, 64), (64, 100, 128)]
-LAST_SECOND_PAIR = 88
+LAST_FIRST_PAIR = [(0, 36, 64), (64, 96, 128)]
+LAST_SECOND_PAIR = 104
 PAIRED_EXPERTS = 5
 OUT_BANKS = [[0], [1, 3], [7, 4], [2]]
 

@@ -31,9 +31,10 @@ SLABS = E * PASSES
 X_TOKENS_VECTOR = 352
 W_COLUMNS_VECTOR = [44] * (SLABS - 2) + [64]
 
-SLOT_PIECES = [(0, 256), (256, 640), (640, 1024)]
+SLOT_PIECES = [(0, 256), (256, 1024)]
+WINDOW = 2 * T
 
-EXPERT_GROUPS = [(0, 4, "vector", 0), (4, 2, "vector", 4), (6, 1, "scalar", 0), (7, 1, "scalar", 4)]
+EXPERT_GROUPS = [(0, 2, "vector", 4), (2, 2, "vector", 0), (4, 2, "vector", 4), (6, 1, "scalar", 0), (7, 1, "scalar", 4)]
 
 TURNED_PIECES = [(0, 256), (256, 384)]
 TURNED = TURNED_PIECES[-1][1]
@@ -69,14 +70,16 @@ def tile_moe_nxt_lin_bias_kernel(
         offs_sb = held.tile([P, SLOTS // 16], U16, name="offs_sb")
         pos_sb = [held.tile([P, T // 16], U16, name=f"pos_sb{i}") for i in range(2)]
 
-        x_scales = held.tile([P, T], U8, name="x_scales", align_bytes=64)
+        x_scales = held.tile([P, WINDOW], U8, name="x_scales", align_bytes=64)
         nc.gpsimd.memset(x_scales[:], 0)
         identity = held.tile([P, P], F32, name="identity")
         make_identity(nc, identity[:])
 
         x_raw = [held.tile([P, PACK, T], F32, name=f"x_raw{a}") for a in range(PASSES)]
         x_cast = [held.tile([P, T * PACK], BF16, name=f"x_cast{a}", align_bytes=64) for a in range(PASSES)]
-        x_codes = [held.tile([P, T], U32, name=f"x_codes{a}", align_bytes=64) for a in range(PASSES)]
+        x_codes = [held.tile([P, WINDOW], U32, name=f"x_codes{a}", align_bytes=64) for a in range(PASSES)]
+        for a in range(PASSES):
+            nc.gpsimd.memset(x_codes[a][:, T:], 0)
         slot_codes = [held.tile([P, SLOTS], U32, name=f"slot_codes{a}", align_bytes=64) for a in range(PASSES)]
         slot_scales = held.tile([P, SLOTS], U8, name="slot_scales", align_bytes=64)
         b_sb = held.tile([P, R, E], F32, name="b_sb")
@@ -99,7 +102,7 @@ def tile_moe_nxt_lin_bias_kernel(
 
         def quantise_x(a):
             nc.vector.quantize_mx(
-                out=x_codes[a][:].bitcast(FP8X4), scales=x_scales[4 * a : P, :], in_=x_cast[a][:]
+                out=x_codes[a][:, :T].bitcast(FP8X4), scales=x_scales[4 * a : P, :T], in_=x_cast[a][:]
             )
 
         def gather_codes(a, slot_piece):

@@ -29,7 +29,7 @@ LINE = 4
 SLABS = E * PASSES
 
 X_TOKENS_VECTOR = 352
-W_COLUMNS_VECTOR = [44] * (SLABS - 2) + [64]
+W_COLUMNS_VECTOR = [44] * (SLABS - 2) + [80]
 
 SLOT_PIECES = [(0, 256), (256, 1024)]
 WINDOW = 2 * T

@@ -215,12 +215,11 @@ def tile_moe_nxt_lin_bias_kernel(
         load_x(1)
         nc.sync.dma_start(out=b_sb[:], in_=b.rearrange("(p r) e -> p r e", r=R))
 
-        dst, src = interleave(x_cast[0][:], x_raw[0][:])
-        split = X_TOKENS_VECTOR // LINE
-        nc.vector.tensor_copy(out=dst[:, :split], in_=src[:, :split])
-        nc.scalar.copy(out=dst[:, split:], in_=src[:, split:])
-        dst, src = interleave(x_cast[1][:], x_raw[1][:])
-        nc.scalar.copy(out=dst, in_=src)
+        dst = [x_cast[a][:].rearrange("p (t j) -> p t j", j=PACK) for a in range(PASSES)]
+        src = [x_raw[a][:].rearrange("p j t -> p t j") for a in range(PASSES)]
+        nc.vector.tensor_copy(out=dst[0][:, :X_TOKENS_VECTOR], in_=src[0][:, :X_TOKENS_VECTOR])
+        nc.scalar.copy(out=dst[0][:, X_TOKENS_VECTOR:], in_=src[0][:, X_TOKENS_VECTOR:])
+        nc.scalar.copy(out=dst[1], in_=src[1])
         for a in range(PASSES):
             quantise_x(a)
         for a in range(PASSES):
@@ -256,6 +255,8 @@ def tile_moe_nxt_lin_bias_kernel(
 
         wp_codes = held.tile([P, M], U32, name="wp_codes", align_bytes=64)
 
+        out_rows = out.rearrange("(p s) t -> p s t", s=2)
+
         def offsets_of(i, lo, hi):
             return pos_sb[i][:, lo // 16 : hi // 16]
 
@@ -282,9 +283,9 @@ def tile_moe_nxt_lin_bias_kernel(
                     )
                 copy[j](out=staged[:, j * per_bank : (j + 1) * per_bank, :], in_=acc[:])
                 if len(numbers) > 1:
-                    nc.sync.dma_start(out=out[j * P : (j + 1) * P, tokens], in_=staged[:, j, :])
+                    nc.sync.dma_start(out=out_rows[:, j, tokens], in_=staged[:, j, :])
             if len(numbers) == 1:
-                nc.sync.dma_start(out=out.rearrange("(f p) t -> p f t", p=P)[:, :, tokens], in_=staged[:])
+                nc.sync.dma_start(out=out_rows[:, :, tokens], in_=staged[:])
 
         def add_rounded(block, first, second):
             grouped = held.tile([P, P * PACK], BF16, name=f"c_cast{block}", align_bytes=64)
@@ -318,8 +319,10 @@ def tile_moe_nxt_lin_bias_kernel(
         for block in range(TURNED // P):
             if block == 1:
                 wp_cast = held.tile([P, M * PACK], BF16, name="wp_cast", tag="plain0", align_bytes=64)
-                dst, src = interleave(wp_cast[:], wp_raw[:])
-                nc.scalar.copy(out=dst, in_=src)
+                nc.scalar.copy(
+                    out=wp_cast[:].rearrange("p (s m j) -> p m j s", s=2, j=PACK),
+                    in_=wp_raw[:].rearrange("p j (m s) -> p m j s", s=2),
+                )
                 nc.vector.quantize_mx(out=wp_codes[:].bitcast(FP8X4), scales=wp_scales[:], in_=wp_cast[:])
             scaled = held.tile([P, R, P], F32, name=f"scaled{block}", align_bytes=64)
             nc.scalar.activation(scaled[:], turned[block][:], COPY, scale=turned_gate[:, block, 0:1])

@@ -146,7 +146,10 @@ def tile_moe_nxt_lin_bias_kernel(
                 nc.scalar.copy(out=dst[:, :LAST_SECOND_PAIR, :, 2:], in_=src[:, :LAST_SECOND_PAIR, :, 2:])
             else:
                 split = W_COLUMNS_VECTOR[slab]
-                nc.vector.tensor_copy(out=dst[:, :split], in_=src[:, :split])
+                nc.vector.tensor_copy(
+                    out=grouped[:].rearrange("p (s u m j) -> p s m j u", s=2, u=2, j=PACK)[:, :, :split],
+                    in_=raw.rearrange("p (j m s u) -> p s m j u", j=PACK, s=2, u=2)[:, :, :split],
+                )
                 nc.scalar.copy(out=dst[:, split:], in_=src[:, split:])
             return grouped
 

from contextlib import ExitStack

import concourse.mybir as mybir
from concourse.masks import make_identity

K, T, E, C, N, M = 1024, 512, 8, 128, 512, 256
SLOTS = E * C

FLOPS = 2 * SLOTS * K * N + 2 * T * N * M
BYTES = 4 * (K * T + E * K * N + N * E + N * M + 2 * T + M * T) + 2 * 8 * 16 * (SLOTS + 2 * T) // 16

F32 = mybir.dt.float32
BF16 = mybir.dt.bfloat16
U32 = mybir.dt.uint32
U16 = mybir.dt.uint16
U8 = mybir.dt.uint8
FP8X4 = mybir.dt.float8_e4m3fn_x4
MULT = mybir.AluOpType.mult
ADD = mybir.AluOpType.add
IDENTITY = mybir.ActivationFunctionType.Identity
COPY = mybir.ActivationFunctionType.Copy

P = 128
PACK = 4
K_PASS = P * PACK
PASSES = K // K_PASS
R = N // P
LINE = 4
SLABS = E * PASSES

X_TOKENS_VECTOR = 352
W_COLUMNS_VECTOR = [44] * (SLABS - 2) + [80]

SLOT_PIECES = [(0, 256), (256, 1024)]
WINDOW = 2 * T

EXPERT_GROUPS = [(0, 2, "vector", 4), (2, 2, "vector", 0), (4, 2, "vector", 4), (6, 1, "scalar", 0), (7, 1, "scalar", 4)]

TURNED_PIECES = [(0, 256), (256, 384)]
TURNED = TURNED_PIECES[-1][1]


LAST_FIRST_PAIR = [(0, 36, 64), (64, 96, 128)]
LAST_SECOND_PAIR = 104
PAIRED_EXPERTS = 5
OUT_BANKS = [[0], [1, 3], [7, 4], [2]]


def interleave(grouped, raw, run=LINE):
    return (
        grouped.rearrange("p (c i j) -> p c j i", i=run, j=PACK),
        raw.rearrange("p j (c i) -> p c j i", i=run),
    )


def tile_moe_nxt_lin_bias_kernel(
    tc, xT, w, b, wp, gate, offs, pos1, pos2, out
):
    nc = tc.nc
    with ExitStack() as ctx:
        held = ctx.enter_context(tc.tile_pool(name="held", bufs=1))
        slab_pool = ctx.enter_context(tc.tile_pool(name="slab_pool", bufs=4))
        cast_pool = ctx.enter_context(tc.tile_pool(name="cast_pool", bufs=3))
        code_pool = ctx.enter_context(tc.tile_pool(name="code_pool", bufs=4))
        banks = ctx.enter_context(tc.psum_pool(name="banks", bufs=1))

        def bank(number, shape):
            return banks.tile(shape, F32, name=f"bank{number}")

        offs_sb = held.tile([P, SLOTS // 16], U16, name="offs_sb")
        pos_sb = [held.tile([P, T // 16], U16, name=f"pos_sb{i}") for i in range(2)]

        x_scales = held.tile([P, WINDOW], U8, name="x_scales", align_bytes=64)
        nc.gpsimd.memset(x_scales[:], 0)
        identity = held.tile([P, P], F32, name="identity")
        make_identity(nc, identity[:])

        x_raw = [held.tile([P, PACK, T], F32, name=f"x_raw{a}") for a in range(PASSES)]
        x_cast = [held.tile([P, T * PACK], BF16, name=f"x_cast{a}", align_bytes=64) for a in range(PASSES)]
        x_codes = [held.tile([P, WINDOW], U32, name=f"x_codes{a}", align_bytes=64) for a in range(PASSES)]
        for a in range(PASSES):
            nc.gpsimd.memset(x_codes[a][:, T:], 0)
        slot_codes = [held.tile([P, SLOTS], U32, name=f"slot_codes{a}", align_bytes=64) for a in range(PASSES)]
        slot_scales = held.tile([P, SLOTS], U8, name="slot_scales", align_bytes=64)
        b_sb = held.tile([P, R, E], F32, name="b_sb")
        first_gate = held.tile([P, T], F32, name="first_gate")
        last_gate = held.tile([P, T - TURNED], F32, name="last_gate")
        turned_gate = held.tile([P, TURNED // P, 8], F32, name="turned_gate")
        wp_raw = held.tile([P, PACK, M], F32, name="wp_raw")
        wp_scales = held.tile([P, M], U8, name="wp_scales", align_bytes=64)
        y = [held.tile([P, SLOTS], F32, name=f"y{r}", align_bytes=64) for r in range(R)]

        def load_x(a):
            rows = xT[a * K_PASS : (a + 1) * K_PASS, :]
            nc.sync.dma_start(out=x_raw[a][:], in_=rows.rearrange("(p j) t -> p j t", j=PACK))

        def load_turned_gate(lo, hi):
            with nc.allow_non_contiguous_dma(reason="one gate value a partition"):
                nc.sync.dma_start(
                    out=turned_gate[:, lo:hi, 0], in_=gate[1, 0, lo * P : hi * P].rearrange("(b t) -> t b", t=P)
                )

        def quantise_x(a):
            nc.vector.quantize_mx(
                out=x_codes[a][:, :T].bitcast(FP8X4), scales=x_scales[4 * a : P, :T], in_=x_cast[a][:]
            )

        def gather_codes(a, slot_piece):
            lo, hi = SLOT_PIECES[slot_piece]
            offsets = offs_sb[:, lo // 16 : hi // 16]
            nc.vector.tensor_copy(out=slot_codes[a][:, lo:hi], in_=x_codes[a][:].indirect(offsets))

        def gather_scales(slot_piece):
            lo, hi = SLOT_PIECES[slot_piece]
            offsets = offs_sb[:, lo // 16 : hi // 16]
            nc.vector.tensor_copy(out=slot_scales[:, lo:hi], in_=x_scales[:].indirect(offsets))

        def load_expert(e):
            if e < PAIRED_EXPERTS:
                raw = slab_pool.tile([P, PASSES, PACK * N], F32, name="w_raw")
                nc.sync.dma_start(out=raw[:], in_=w[e].rearrange("(a p j) n -> p a (j n)", a=PASSES, j=PACK))
                return raw
            slabs = []
            for a in range(PASSES):
                raw = slab_pool.tile([P, PACK * N], F32, name="w_raw_slab")
                rows = w[e, a * K_PASS : (a + 1) * K_PASS, :]
                rows = rows.rearrange("(p j) n -> p (j n)", j=PACK)
                if e * PASSES + a == SLABS - 1:
                    cut = PACK * N - N // 2
                    nc.sync.dma_start(out=raw[:, :cut], in_=rows[:, :cut])
                    nc.sync.dma_start(out=raw[:, cut:], in_=rows[:, cut:])
                else:
                    nc.sync.dma_start(out=raw[:], in_=rows)
                slabs.append(raw[:])
            return slabs

        def cast_slab(slab, raw):
            grouped = cast_pool.tile([P, N * PACK], BF16, name="w_cast", align_bytes=64)
            dst = grouped[:].rearrange("p (r m j) -> p m j r", r=R, j=PACK)
            src = raw.rearrange("p (j m r) -> p m j r", j=PACK, r=R)
            if slab == SLABS - 1:
                for lo, mid, hi in LAST_FIRST_PAIR:
                    nc.vector.tensor_copy(out=dst[:, lo:mid, :, :2], in_=src[:, lo:mid, :, :2])
                    nc.scalar.copy(out=dst[:, mid:hi, :, :2], in_=src[:, mid:hi, :, :2])
                nc.vector.tensor_copy(out=dst[:, LAST_SECOND_PAIR:, :, 2:], in_=src[:, LAST_SECOND_PAIR:, :, 2:])
                nc.scalar.copy(out=dst[:, :LAST_SECOND_PAIR, :, 2:], in_=src[:, :LAST_SECOND_PAIR, :, 2:])
            else:
                split = W_COLUMNS_VECTOR[slab]
                nc.vector.tensor_copy(
                    out=grouped[:].rearrange("p (s u m j) -> p s m j u", s=2, u=2, j=PACK)[:, :, :split],
                    in_=raw.rearrange("p (j m s u) -> p s m j u", j=PACK, s=2, u=2)[:, :, :split],
                )
                nc.scalar.copy(out=dst[:, split:], in_=src[:, split:])
            return grouped

        def quantise_slab(slab, grouped):
            codes = code_pool.tile([P, N], U32, name="w_codes", align_bytes=64)
            scales = code_pool.tile([P, N], U8, name="w_scales", align_bytes=64)
            parts = R if slab == SLABS - 1 else 1
            for part in range(parts):
                lo, hi = part * N // parts, (part + 1) * N // parts
                nc.vector.quantize_mx(
                    out=codes[:, lo:hi].bitcast(FP8X4),
                    scales=scales[:, lo:hi],
                    in_=grouped[:, lo * PACK : hi * PACK],
                )
            return codes, scales

        def cast_expert(raw):
            grouped = cast_pool.tile([P, PASSES * N * PACK], BF16, name="w_cast_expert", align_bytes=64, bufs=2)
            dst = grouped[:].rearrange("p (a r m j) -> p a m j r", a=PASSES, r=R, j=PACK)
            src = raw[:].rearrange("p a (j m r) -> p a m j r", j=PACK, r=R)
            split = W_COLUMNS_VECTOR[0]
            nc.vector.tensor_copy(out=dst[:, :, :split], in_=src[:, :, :split])
            nc.scalar.copy(out=dst[:, :, split:], in_=src[:, :, split:])
            return grouped

        def quantise_expert(grouped):
            codes = code_pool.tile([P, PASSES * N], U32, name="w_codes_expert", align_bytes=64, bufs=2)
            scales = code_pool.tile([P, PASSES * N], U8, name="w_scales_expert", align_bytes=64, bufs=2)
            nc.vector.quantize_mx(out=codes[:].bitcast(FP8X4), scales=scales[:], in_=grouped[:])
            return [(codes[:, a * N : (a + 1) * N], scales[:, a * N : (a + 1) * N]) for a in range(PASSES)]

        def multiply(e, slabs, group_banks, place):
            slots = slice(e * C, (e + 1) * C)
            for r in range(R):
                for a, (codes, scales) in enumerate(slabs):
                    nc.tensor.matmul_mx(
                        out=group_banks[r][:, place, :],
                        lhsT=codes[:, r * P : (r + 1) * P].bitcast(FP8X4),
                        lhsT_scale=scales[:, r * P : (r + 1) * P],
                        rhs=slot_codes[a][:, slots].bitcast(FP8X4),
                        rhs_scale=slot_scales[4 * a : P, slots],
                        start=(a == 0),
                        stop=(a == PASSES - 1),
                    )

        def copy_out(first, experts, engine, group_banks):
            for r in range(R):
                if engine == "vector":
                    results = y[r][:, first * C : (first + experts) * C]
                    bias = b_sb[:, r, first : first + experts].unsqueeze(2).to_broadcast([P, experts, C])
                    nc.vector.tensor_tensor(
                        results.rearrange("p (e c) -> p e c", e=experts), group_banks[r][:], bias, ADD
                    )
                else:
                    for i in range(experts):
                        e = first + i
                        nc.scalar.activation(
                            y[r][:, e * C : (e + 1) * C],
                            group_banks[r][:, i, :],
                            IDENTITY,
                            bias=b_sb[:, r, e : e + 1],
                        )

        load_x(0)
        nc.sync.dma_start(offs_sb[:], offs)
        load_x(1)
        nc.sync.dma_start(out=b_sb[:], in_=b.rearrange("(p r) e -> p r e", r=R))

        dst = [x_cast[a][:].rearrange("p (t j) -> p t j", j=PACK) for a in range(PASSES)]
        src = [x_raw[a][:].rearrange("p j t -> p t j") for a in range(PASSES)]
        nc.vector.tensor_copy(out=dst[0][:, :X_TOKENS_VECTOR], in_=src[0][:, :X_TOKENS_VECTOR])
        nc.scalar.copy(out=dst[0][:, X_TOKENS_VECTOR:], in_=src[0][:, X_TOKENS_VECTOR:])
        nc.scalar.copy(out=dst[1], in_=src[1])
        for a in range(PASSES):
            quantise_x(a)
        for a in range(PASSES):
            gather_codes(a, 0)
        gather_scales(0)

        for first, experts, engine, first_bank in EXPERT_GROUPS:
            group_banks = []
            for place in range(experts):
                e = first + place
                raws = load_expert(e)
                if e == E - 1:
                    for i, pos in enumerate((pos1, pos2)):
                        nc.sync.dma_start(pos_sb[i][:], pos)
                    nc.sync.dma_start(out=first_gate[:], in_=gate[0, 0:P, :])
                    load_turned_gate(0, 1)
                    nc.sync.dma_start(out=last_gate[:], in_=gate[1, 0:P, TURNED:])
                    nc.sync.dma_start(out=wp_raw[:], in_=wp.rearrange("(p j) f -> p j f", j=PACK))
                    load_turned_gate(1, TURNED // P)
                if e < PAIRED_EXPERTS:
                    slabs = quantise_expert(cast_expert(raws))
                else:
                    slabs = [quantise_slab(e * PASSES + a, cast_slab(e * PASSES + a, raws[a])) for a in range(PASSES)]
                slot_piece = 1 + e
                if slot_piece < len(SLOT_PIECES):
                    for a in range(PASSES):
                        gather_codes(a, slot_piece)
                    gather_scales(slot_piece)
                if place == 0:
                    group_banks = [bank(first_bank + r, [P, experts, C]) for r in range(R)]
                multiply(e, slabs, group_banks, place)
            copy_out(first, experts, engine, group_banks)

        wp_codes = held.tile([P, M], U32, name="wp_codes", align_bytes=64)

        out_rows = out.rearrange("(p s) t -> p s t", s=2)

        def offsets_of(i, lo, hi):
            return pos_sb[i][:, lo // 16 : hi // 16]

        def project(block, grouped, place_of_codes, copy):
            codes = held.tile([P, P], U32, name=f"c_codes{block}", tag=place_of_codes, align_bytes=64)
            scales = held.tile([P, P], U8, name=f"c_scales{block}", align_bytes=64)
            nc.vector.quantize_mx(out=codes[:].bitcast(FP8X4), scales=scales[:], in_=grouped)
            staged = held.tile([P, M // P, P], F32, name=f"staged{block}")
            tokens = slice(block * P, (block + 1) * P)
            numbers = OUT_BANKS[block]
            per_bank = M // P // len(numbers)
            for j, number in enumerate(numbers):
                acc = bank(number, [P, per_bank, P])
                for place in range(per_bank):
                    f = j * per_bank + place
                    nc.tensor.matmul_mx(
                        out=acc[:, place, :],
                        lhsT=wp_codes[:, f * P : (f + 1) * P].bitcast(FP8X4),
                        lhsT_scale=wp_scales[:, f * P : (f + 1) * P],
                        rhs=codes[:].bitcast(FP8X4),
                        rhs_scale=scales[:],
                        start=True,
                        stop=True,
                    )
                copy[j](out=staged[:, j * per_bank : (j + 1) * per_bank, :], in_=acc[:])
                if len(numbers) > 1:
                    nc.sync.dma_start(out=out_rows[:, j, tokens], in_=staged[:, j, :])
            if len(numbers) == 1:
                nc.sync.dma_start(out=out_rows[:, :, tokens], in_=staged[:])

        def add_rounded(block, first, second):
            grouped = held.tile([P, P * PACK], BF16, name=f"c_cast{block}", align_bytes=64)
            dst, first = interleave(grouped[:], first, run=2)
            nc.vector.tensor_tensor(dst, first, interleave(grouped[:], second, run=2)[1], ADD)
            return grouped

        first_product = held.tile([P, R, T], F32, name="first_product", tag="x_raw0")
        for r in range(R):
            nc.vector.tensor_tensor(
                first_product[:, r, :], y[r][:].indirect(offsets_of(0, 0, T)), first_gate[:], MULT
            )
        last_product = held.tile([P, R, T - TURNED], F32, name="last_product")
        for r in range(R):
            nc.vector.tensor_tensor(
                last_product[:, r, :], y[r][:].indirect(offsets_of(1, TURNED, T)), last_gate[:], MULT
            )

        turned = []
        for k, (lo, hi) in enumerate(TURNED_PIECES):
            plain = held.tile([P, R, hi - lo], F32, name=f"plain{k}", align_bytes=64)
            blocks = range(lo // P, hi // P)
            for block in blocks:
                turned.append(bank(block, [P, R, P]))
            for r in range(R):
                nc.scalar.activation(plain[:, r, :], y[r][:].indirect(offsets_of(1, lo, hi)), COPY)
                for block in blocks:
                    tokens = slice(block * P - lo, (block + 1) * P - lo)
                    nc.tensor.transpose(turned[block][:, r, :], plain[:, r, tokens], identity[:])
        second_product = []
        for block in range(TURNED // P):
            if block == 1:
                wp_cast = held.tile([P, M * PACK], BF16, name="wp_cast", tag="plain0", align_bytes=64)
                nc.scalar.copy(
                    out=wp_cast[:].rearrange("p (s m j) -> p m j s", s=2, j=PACK),
                    in_=wp_raw[:].rearrange("p j (m s) -> p m j s", s=2),
                )
                nc.vector.quantize_mx(out=wp_codes[:].bitcast(FP8X4), scales=wp_scales[:], in_=wp_cast[:])
            scaled = held.tile([P, R, P], F32, name=f"scaled{block}", align_bytes=64)
            nc.scalar.activation(scaled[:], turned[block][:], COPY, scale=turned_gate[:, block, 0:1])
            back = bank(4 + block, [P, R, P])
            for r in range(R):
                nc.tensor.transpose(back[:, r, :], scaled[:, r, :], identity[:])
            second_product.append(back)


        last_block = T // P - 1
        waiting = (last_block, add_rounded(last_block, last_product[:], first_product[:, :, TURNED:]))
        for block in range(TURNED // P):
            grouped = add_rounded(block, second_product[block][:], first_product[:, :, block * P : (block + 1) * P])
            project(waiting[0], waiting[1][:], f"scaled{block}" if block else "first_codes", [nc.scalar.copy] * 2)
            waiting = (block, grouped)
        project(waiting[0], waiting[1][:], "last_codes", [nc.vector.tensor_copy, nc.scalar.copy])
